import numpy as np
import ml_dtypes


def mxq(x, axis, fmt="e4m3"):
    dtype, down = {"e4m3": (ml_dtypes.float8_e4m3fn, 7), "e5m2": (ml_dtypes.float8_e5m2, 14)}[fmt]
    v = np.moveaxis(np.asarray(x, np.float32).astype(ml_dtypes.bfloat16).astype(np.float64), axis, -1)
    blocks = v.reshape(v.shape[:-1] + (-1, 32))
    amax = np.abs(blocks).max(-1, keepdims=True)
    byte = np.maximum(np.where(amax > 0, np.frexp(amax)[1] - 1 + 127, 0) - down, 1)
    scale = np.exp2(byte - 127.0)
    codes = (blocks / scale).astype(np.float32).astype(dtype).astype(np.float64)
    return np.moveaxis((codes * scale).reshape(v.shape), -1, axis)


WIDE = False


def mx_kscale(k):
    if not WIDE:
        return np.ones(k)
    levels = np.array([10, -10, 5, -5, 0])
    if k % 512:
        return np.exp2(np.random.permutation(np.resize(levels, k // 32))).repeat(32)
    a = np.empty((k // 512, 16))
    for p in range(k // 512):
        a[p, :8] = np.random.permutation(np.resize(levels, 8))
        for g in range(8):
            far = levels[np.abs(levels - a[p, g]) >= 10]
            a[p, g + 8] = far[np.random.randint(len(far))]
    return np.exp2(a.ravel()).repeat(32)


def f64(x):
    return np.asarray(x).astype(np.float64)


def striped(idx):
    return np.tile(idx.reshape(-1, 16).T, (8, 1)).astype(np.uint16)


def unstriped(offs):
    return offs[:16].T.reshape(-1).astype(np.int64)


def pack_weight(w):
    k, n = w.shape
    w = f64(np.asarray(w, np.float32).astype(ml_dtypes.bfloat16)).reshape(k // 32, 32, n)
    amax = np.abs(w).max(1)
    byte = np.clip(np.where(amax > 0, np.frexp(amax)[1] - 1 + 127 - 7, 1), 1, 254)
    scaled = (w * np.exp2(127.0 - byte)[:, None, :]).reshape(k, n).astype(np.float32)
    words = np.ascontiguousarray(scaled.reshape(k // 512, 128, 4, n).transpose(0, 1, 3, 2)).astype(ml_dtypes.float8_e4m3fn).view(np.uint8)
    return words, np.ascontiguousarray(byte.astype(np.uint8).reshape(k // 512, 16, n))


def unpack_weight(words, scales):
    g, p, n, _ = words.shape
    vals = np.ascontiguousarray(words).view(ml_dtypes.float8_e4m3fn).astype(np.float64) * np.repeat(np.exp2(scales.astype(np.float64) - 127.0), 8, axis=1)[..., None]
    return vals.transpose(0, 1, 3, 2).reshape(g * 512, n)


def relu(v):
    return np.maximum(v, 0.0)


K, T, S, N = 1536, 2048, 768, 256


def setup_inputs():
    n = np.random.standard_normal
    s = mx_kscale(K)[:, None]
    words, scales = pack_weight(n((K, N)) / np.sqrt(K) / s)
    return {
        "xT": (n((K, T)) * s).astype(np.float32),
        "w_words": words,
        "w_scales": scales,
        "b": (0.3 * n((N, 1))).astype(np.float32),
        "offs": striped(np.random.permutation(T)[:S]),
    }


def reference(xT, w_words, w_scales, b, offs):
    w = unpack_weight(w_words, w_scales)
    idx = unstriped(offs)
    xq = mxq(f64(xT)[:, idx], 0, "e4m3")
    y = w.T @ xq
    y = relu(y + f64(b))
    return y

@@ -1,0 +1,171 @@
+from contextlib import ExitStack
+
+import concourse.mybir as mybir
+
+K, T, S, N = 1536, 2048, 768, 256
+FLOPS = 2 * K * S * N
+
+F32 = mybir.dt.float32
+BF16 = mybir.dt.bfloat16
+I32 = mybir.dt.int32
+U32 = mybir.dt.uint32
+U16 = mybir.dt.uint16
+U8 = mybir.dt.uint8
+FP8X4 = mybir.dt.float8_e4m3fn_x4
+COPY = mybir.ActivationFunctionType.Copy
+RELU = mybir.ActivationFunctionType.Relu
+ADD = mybir.AluOpType.add
+MAX = mybir.AluOpType.max
+
+P = 128
+PACK = 4
+PASSES = K // (P * PACK)
+SLICE = 256
+SLICES = S // SLICE
+M_TILES = N // P
+PER_COL = 16
+
+
+def tile_picked_pick_lin_relu_sub_e_kernel(tc, xT, w_words, w_scales, b, offs, out):
+    nc = tc.nc
+    last = PASSES - 1
+    with ExitStack() as ctx:
+        keep = ctx.enter_context(tc.tile_pool(name="keep", bufs=1))
+        psum = ctx.enter_context(tc.psum_pool(name="psum", bufs=1))
+
+        offsets = keep.tile([P, S // PER_COL], U16, name="offsets")
+        planes = [
+            [keep.tile([P, T], F32, name=f"plane{a}_{t}", align_bytes=64) for t in range(PACK)] for a in range(PASSES)
+        ]
+        w_codes = [keep.tile([P, N], U32, name=f"w_codes{a}", align_bytes=64) for a in range(PASSES)]
+        w_scale = keep.tile([P, N], U8, name="w_scale", align_bytes=64)
+        bias = keep.tile([P, M_TILES], F32, name="bias")
+        warm = keep.tile([P, 8], F32, name="warm")
+        warm_out = keep.tile([P, 8], F32, name="warm_out")
+
+        x_rows = xT.rearrange("(a p t) n -> a t p n", p=P, t=PACK)
+
+        def load_plane(a, t):
+            nc.sync.dma_start(out=planes[a][t][:], in_=x_rows[a, t])
+
+        def load_codes(a):
+            nc.sync.dma_start(
+                out=w_codes[a][:].bitcast(I32),
+                in_=w_words[a].rearrange("p m r -> p (m r)").bitcast(I32),
+            )
+
+        nc.vector.memset(w_scale[:].bitcast(I32), 0)
+        nc.vector.memset(warm[:], 0.0)
+
+        load_plane(0, 0)
+        nc.sync.dma_start(offsets[:], offs)
+        load_plane(0, 1)
+        load_plane(0, 2)
+        for q in range(4):
+            nc.scalar.dma_start(
+                out=w_scale[32 * q : 32 * q + 4 * PASSES, :].bitcast(I32),
+                in_=w_scales[:, 4 * q : 4 * q + 4, :].bitcast(I32),
+            )
+        nc.scalar.activation(warm_out[:], warm[:], RELU)
+        load_plane(0, 3)
+        for t in range(PACK):
+            load_plane(1, t)
+        for t in range(PACK - 1):
+            load_plane(last, t)
+        load_codes(0)
+        load_plane(last, PACK - 1)
+        load_codes(1)
+        load_codes(2)
+        with nc.allow_non_contiguous_dma(reason="one bias value a partition and output tile"):
+            nc.sync.dma_start(out=bias[:], in_=b.rearrange("(c p) o -> p (c o)", p=P))
+
+        low = [keep.tile([P, 2, S], F32, name=f"low{a}") for a in range(PASSES)]
+        high_head = [keep.tile([P, 2, SLICE], F32, name=f"high_head{a}", align_bytes=64) for a in range(PASSES)]
+        high_rest = [keep.tile([P, 2, S - SLICE], F32, name=f"high_rest{a}") for a in range(PASSES)]
+        grouped = [keep.tile([P, S, PACK], BF16, name=f"grouped{a}", align_bytes=64) for a in range(PASSES)]
+        x_scale = [keep.tile([P, S], U8, name=f"x_scale{a}", align_bytes=64) for a in range(PASSES)]
+        x_codes = {}
+        acc = [[psum.tile([P, SLICE], F32, name=f"acc{s}_{m}") for m in range(M_TILES)] for s in range(SLICES)]
+        result = [[keep.tile([P, SLICE], F32, name=f"result{s}_{m}") for m in range(M_TILES)] for s in range(SLICES)]
+        direct = SLICES - 1
+        nc.vector.memset(high_rest[last][:, 1, (direct - 1) * SLICE : direct * SLICE], 0.0)
+
+        def span(s0, s1):
+            return slice(s0 * SLICE, s1 * SLICE)
+
+        def picked(a, u, s0, s1):
+            if u == 0:
+                return low[a][:, :, span(s0, s1)]
+            if s0 == 0:
+                return high_head[a][:]
+            return high_rest[a][:, :, span(s0 - 1, s1 - 1)]
+
+        def window(a, t, s0, s1):
+            return planes[a][t][:].indirect(offsets[:, s0 * SLICE // PER_COL : s1 * SLICE // PER_COL])
+
+        def gather(a, t, s0, s1):
+            nc.vector.tensor_copy(picked(a, t // 2, s0, s1)[:, t % 2, :], window(a, t, s0, s1))
+
+        def interleave(a, u, s0, s1):
+            src = picked(a, u, s0, s1).rearrange("p t n -> p n t")
+            nc.scalar.activation(grouped[a][:, span(s0, s1), 2 * u : 2 * u + 2], src, COPY)
+
+        def quantize(a, s0, s1, tag):
+            codes = keep.tile([P, (s1 - s0) * SLICE], U32, name=f"x_codes{a}_{s0}", tag=tag, align_bytes=64)
+            for s in range(s0, s1):
+                x_codes[a, s] = codes[:, span(s - s0, s - s0 + 1)]
+            nc.vector.quantize_mx(
+                out=codes[:].bitcast(FP8X4),
+                scales=x_scale[a][:, span(s0, s1)],
+                in_=grouped[a][:, span(s0, s1), :].rearrange("p n t -> p (n t)"),
+            )
+
+        def multiply(a, s):
+            for m in range(M_TILES):
+                cols = slice(m * P, (m + 1) * P)
+                nc.tensor.matmul_mx(
+                    out=acc[s][m][:],
+                    lhsT=w_codes[a][:, cols].bitcast(FP8X4),
+                    lhsT_scale=w_scale[4 * a : P, cols],
+                    rhs=x_codes[a, s].bitcast(FP8X4),
+                    rhs_scale=x_scale[a][:, span(s, s + 1)],
+                    start=(a == 0),
+                    stop=(a == last),
+                )
+
+        def finish(s):
+            nc.scalar.activation(result[s][0][:], acc[s][0][:], RELU, bias=bias[:, 0:1])
+            nc.vector.tensor_scalar(result[s][1][:], acc[s][1][:], bias[:, 1:2], 0.0, ADD, MAX)
+            for m in range(M_TILES):
+                nc.sync.dma_start(out=out[m * P : (m + 1) * P, span(s, s + 1)], in_=result[s][m][:])
+
+        for a in range(PASSES):
+            gather(a, 0, 0, SLICES)
+            if a > 0:
+                quantize(a - 1, 1, SLICES, f"plane{a}_0")
+            gather(a, 1, 0, SLICES)
+            interleave(a, 0, 0, SLICES)
+            gather(a, 2, 0, 1)
+            gather(a, 2, 1, SLICES)
+            if a < last:
+                for s in range(SLICES):
+                    gather(a, 3, s, s + 1)
+                    interleave(a, 1, s, s + 1)
+                quantize(a, 0, 1, f"x_codes{a}_0")
+
+        interleave(last, 1, direct, SLICES)
+        for a in range(last):
+            for s in range(SLICES):
+                multiply(a, s)
+        for s in range(direct):
+            gather(last, 3, s, s + 1)
+            interleave(last, 1, s, s + 1)
+        nc.vector.tensor_copy(grouped[last][:, span(direct, SLICES), 3], window(last, 3, direct, SLICES))
+        quantize(last, 0, 1, "x_codes_first")
+        quantize(last, 2, 3, f"high_head{last}")
+        quantize(last, 1, 2, "x_codes_last")
+        order = [0, 2, 1]
+        for s in order:
+            multiply(last, s)
+        for s in order:
+            finish(s)

@@ -31,7 +31,7 @@ def tile_picked_pick_lin_relu_sub_e_kernel(tc, xT, w_words, w_scales, b, offs, o
     last = PASSES - 1
     with ExitStack() as ctx:
         keep = ctx.enter_context(tc.tile_pool(name="keep", bufs=1))
-        psum = ctx.enter_context(tc.psum_pool(name="psum", bufs=1))
+        psum = ctx.enter_context(tc.psum_pool(name="psum", bufs=2))
 
         offsets = keep.tile([P, S // PER_COL], U16, name="offsets")
         planes = [
@@ -59,23 +59,18 @@ def tile_picked_pick_lin_relu_sub_e_kernel(tc, xT, w_words, w_scales, b, offs, o
 
         load_plane(0, 0)
         nc.sync.dma_start(offsets[:], offs)
-        load_plane(0, 1)
-        load_plane(0, 2)
+        nc.scalar.activation(warm_out[:], warm[:], RELU)
+        for a in range(PASSES):
+            for t in range(PACK):
+                if (a, t) != (0, 0):
+                    load_plane(a, t)
         for q in range(4):
-            nc.scalar.dma_start(
+            nc.sync.dma_start(
                 out=w_scale[32 * q : 32 * q + 4 * PASSES, :].bitcast(I32),
                 in_=w_scales[:, 4 * q : 4 * q + 4, :].bitcast(I32),
             )
-        nc.scalar.activation(warm_out[:], warm[:], RELU)
-        load_plane(0, 3)
-        for t in range(PACK):
-            load_plane(1, t)
-        for t in range(PACK - 1):
-            load_plane(last, t)
-        load_codes(0)
-        load_plane(last, PACK - 1)
-        load_codes(1)
-        load_codes(2)
+        for a in range(PASSES):
+            load_codes(a)
         with nc.allow_non_contiguous_dma(reason="one bias value a partition and output tile"):
             nc.sync.dma_start(out=bias[:], in_=b.rearrange("(c p) o -> p (c o)", p=P))
 
@@ -85,10 +80,9 @@ def tile_picked_pick_lin_relu_sub_e_kernel(tc, xT, w_words, w_scales, b, offs, o
         grouped = [keep.tile([P, S, PACK], BF16, name=f"grouped{a}", align_bytes=64) for a in range(PASSES)]
         x_scale = [keep.tile([P, S], U8, name=f"x_scale{a}", align_bytes=64) for a in range(PASSES)]
         x_codes = {}
-        acc = [[psum.tile([P, SLICE], F32, name=f"acc{s}_{m}") for m in range(M_TILES)] for s in range(SLICES)]
+        acc = {}
         result = [[keep.tile([P, SLICE], F32, name=f"result{s}_{m}") for m in range(M_TILES)] for s in range(SLICES)]
         direct = SLICES - 1
-        nc.vector.memset(high_rest[last][:, 1, (direct - 1) * SLICE : direct * SLICE], 0.0)
 
         def span(s0, s1):
             return slice(s0 * SLICE, s1 * SLICE)
@@ -120,11 +114,15 @@ def tile_picked_pick_lin_relu_sub_e_kernel(tc, xT, w_words, w_scales, b, offs, o
                 in_=grouped[a][:, span(s0, s1), :].rearrange("p n t -> p (n t)"),
             )
 
-        def multiply(a, s):
-            for m in range(M_TILES):
-                cols = slice(m * P, (m + 1) * P)
+        def gather_grouped(a, t, s):
+            nc.vector.tensor_copy(grouped[a][:, span(s, s + 1), t], window(a, t, s, s + 1))
+
+        def multiply(s, m):
+            cols = slice(m * P, (m + 1) * P)
+            acc[s, m] = psum.tile([P, SLICE], F32, name=f"acc{s}_{m}", tag=f"acc{m}")
+            for a in range(PASSES):
                 nc.tensor.matmul_mx(
-                    out=acc[s][m][:],
+                    out=acc[s, m][:],
                     lhsT=w_codes[a][:, cols].bitcast(FP8X4),
                     lhsT_scale=w_scale[4 * a : P, cols],
                     rhs=x_codes[a, s].bitcast(FP8X4),
@@ -134,8 +132,8 @@ def tile_picked_pick_lin_relu_sub_e_kernel(tc, xT, w_words, w_scales, b, offs, o
                 )
 
         def finish(s):
-            nc.scalar.activation(result[s][0][:], acc[s][0][:], RELU, bias=bias[:, 0:1])
-            nc.vector.tensor_scalar(result[s][1][:], acc[s][1][:], bias[:, 1:2], 0.0, ADD, MAX)
+            nc.scalar.activation(result[s][0][:], acc[s, 0][:], RELU, bias=bias[:, 0:1])
+            nc.vector.tensor_scalar(result[s][1][:], acc[s, 1][:], bias[:, 1:2], 0.0, ADD, MAX)
             for m in range(M_TILES):
                 nc.sync.dma_start(out=out[m * P : (m + 1) * P, span(s, s + 1)], in_=result[s][m][:])
 
@@ -146,26 +144,23 @@ def tile_picked_pick_lin_relu_sub_e_kernel(tc, xT, w_words, w_scales, b, offs, o
             gather(a, 1, 0, SLICES)
             interleave(a, 0, 0, SLICES)
             gather(a, 2, 0, 1)
-            gather(a, 2, 1, SLICES)
             if a < last:
+                gather(a, 2, 1, SLICES)
                 for s in range(SLICES):
                     gather(a, 3, s, s + 1)
                     interleave(a, 1, s, s + 1)
                 quantize(a, 0, 1, f"x_codes{a}_0")
 
-        interleave(last, 1, direct, SLICES)
-        for a in range(last):
-            for s in range(SLICES):
-                multiply(a, s)
+        gather(last, 2, 1, direct)
+        gather_grouped(last, 2, direct)
         for s in range(direct):
             gather(last, 3, s, s + 1)
             interleave(last, 1, s, s + 1)
-        nc.vector.tensor_copy(grouped[last][:, span(direct, SLICES), 3], window(last, 3, direct, SLICES))
+        gather_grouped(last, 3, direct)
         quantize(last, 0, 1, "x_codes_first")
         quantize(last, 2, 3, f"high_head{last}")
         quantize(last, 1, 2, "x_codes_last")
-        order = [0, 2, 1]
-        for s in order:
-            multiply(last, s)
-        for s in order:
+        for s in [0, 2, 1]:
+            for m in range(M_TILES):
+                multiply(s, m)
             finish(s)

@@ -31,7 +31,7 @@ def tile_picked_pick_lin_relu_sub_e_kernel(tc, xT, w_words, w_scales, b, offs, o
     last = PASSES - 1
     with ExitStack() as ctx:
         keep = ctx.enter_context(tc.tile_pool(name="keep", bufs=1))
-        psum = ctx.enter_context(tc.psum_pool(name="psum", bufs=2))
+        psum = ctx.enter_context(tc.psum_pool(name="psum", bufs=1))
 
         offsets = keep.tile([P, S // PER_COL], U16, name="offsets")
         planes = [
@@ -62,13 +62,15 @@ def tile_picked_pick_lin_relu_sub_e_kernel(tc, xT, w_words, w_scales, b, offs, o
         nc.scalar.activation(warm_out[:], warm[:], RELU)
         for a in range(PASSES):
             for t in range(PACK):
-                if (a, t) != (0, 0):
+                if (a, t) not in ((0, 0), (last, PACK - 1)):
                     load_plane(a, t)
+        nc.sync.dma_start(out=planes[last][PACK - 1][:, : T // 2], in_=x_rows[last, PACK - 1][:, : T // 2])
         for q in range(4):
             nc.sync.dma_start(
                 out=w_scale[32 * q : 32 * q + 4 * PASSES, :].bitcast(I32),
                 in_=w_scales[:, 4 * q : 4 * q + 4, :].bitcast(I32),
             )
+        nc.sync.dma_start(out=planes[last][PACK - 1][:, T // 2 :], in_=x_rows[last, PACK - 1][:, T // 2 :])
         for a in range(PASSES):
             load_codes(a)
         with nc.allow_non_contiguous_dma(reason="one bias value a partition and output tile"):
@@ -80,8 +82,11 @@ def tile_picked_pick_lin_relu_sub_e_kernel(tc, xT, w_words, w_scales, b, offs, o
         grouped = [keep.tile([P, S, PACK], BF16, name=f"grouped{a}", align_bytes=64) for a in range(PASSES)]
         x_scale = [keep.tile([P, S], U8, name=f"x_scale{a}", align_bytes=64) for a in range(PASSES)]
         x_codes = {}
-        acc = {}
-        result = [[keep.tile([P, SLICE], F32, name=f"result{s}_{m}") for m in range(M_TILES)] for s in range(SLICES)]
+        acc = {
+            (s, m): psum.tile([P, SLICE], F32, name=f"acc{s}_{m}") for s in range(SLICES) for m in range(M_TILES)
+        }
+        wide_codes = {}
+        result = [keep.tile([P, S], F32, name=f"result{m}") for m in range(M_TILES)]
         direct = SLICES - 1
 
         def span(s0, s1):
@@ -106,6 +111,7 @@ def tile_picked_pick_lin_relu_sub_e_kernel(tc, xT, w_words, w_scales, b, offs, o
 
         def quantize(a, s0, s1, tag):
             codes = keep.tile([P, (s1 - s0) * SLICE], U32, name=f"x_codes{a}_{s0}", tag=tag, align_bytes=64)
+            wide_codes[a, s0] = codes
             for s in range(s0, s1):
                 x_codes[a, s] = codes[:, span(s - s0, s - s0 + 1)]
             nc.vector.quantize_mx(
@@ -117,10 +123,9 @@ def tile_picked_pick_lin_relu_sub_e_kernel(tc, xT, w_words, w_scales, b, offs, o
         def gather_grouped(a, t, s):
             nc.vector.tensor_copy(grouped[a][:, span(s, s + 1), t], window(a, t, s, s + 1))
 
-        def multiply(s, m):
-            cols = slice(m * P, (m + 1) * P)
-            acc[s, m] = psum.tile([P, SLICE], F32, name=f"acc{s}_{m}", tag=f"acc{m}")
-            for a in range(PASSES):
+        def multiply(a, s):
+            for m in range(M_TILES):
+                cols = slice(m * P, (m + 1) * P)
                 nc.tensor.matmul_mx(
                     out=acc[s, m][:],
                     lhsT=w_codes[a][:, cols].bitcast(FP8X4),
@@ -132,10 +137,12 @@ def tile_picked_pick_lin_relu_sub_e_kernel(tc, xT, w_words, w_scales, b, offs, o
                 )
 
         def finish(s):
-            nc.scalar.activation(result[s][0][:], acc[s, 0][:], RELU, bias=bias[:, 0:1])
-            nc.vector.tensor_scalar(result[s][1][:], acc[s, 1][:], bias[:, 1:2], 0.0, ADD, MAX)
+            nc.scalar.activation(result[0][:, span(s, s + 1)], acc[s, 0][:], RELU, bias=bias[:, 0:1])
+            nc.vector.tensor_scalar(result[1][:, span(s, s + 1)], acc[s, 1][:], bias[:, 1:2], 0.0, ADD, MAX)
+
+        def store(s0, s1):
             for m in range(M_TILES):
-                nc.sync.dma_start(out=out[m * P : (m + 1) * P, span(s, s + 1)], in_=result[s][m][:])
+                nc.sync.dma_start(out=out[m * P : (m + 1) * P, span(s0, s1)], in_=result[m][:, span(s0, s1)])
 
         for a in range(PASSES):
             gather(a, 0, 0, SLICES)
@@ -160,7 +167,22 @@ def tile_picked_pick_lin_relu_sub_e_kernel(tc, xT, w_words, w_scales, b, offs, o
         quantize(last, 0, 1, "x_codes_first")
         quantize(last, 2, 3, f"high_head{last}")
         quantize(last, 1, 2, "x_codes_last")
-        for s in [0, 2, 1]:
-            for m in range(M_TILES):
-                multiply(s, m)
+        for i in range(2):
+            spare = psum.tile([P, 2 * SLICE], F32, name=f"spare{i}")
+            nc.tensor.matmul_mx(
+                out=spare[:],
+                lhsT=x_codes[0, 0][:, 0:P].bitcast(FP8X4),
+                lhsT_scale=w_scale[:, 0:P],
+                rhs=wide_codes[0, 1][:].bitcast(FP8X4),
+                rhs_scale=x_scale[0][:, span(1, SLICES)],
+                start=True,
+                stop=True,
+            )
+        order = [0, 2, 1]
+        for a in range(PASSES):
+            for s in order:
+                multiply(a, s)
+        for s in order:
             finish(s)
+        store(0, 1)
+        store(1, SLICES)

@@ -24,6 +24,7 @@ SLICE = 256
 SLICES = S // SLICE
 M_TILES = N // P
 PER_COL = 16
+CUT = 640
 
 
 def tile_picked_pick_lin_relu_sub_e_kernel(tc, xT, w_words, w_scales, b, offs, out):
@@ -64,13 +65,13 @@ def tile_picked_pick_lin_relu_sub_e_kernel(tc, xT, w_words, w_scales, b, offs, o
             for t in range(PACK):
                 if (a, t) not in ((0, 0), (last, PACK - 1)):
                     load_plane(a, t)
-        nc.sync.dma_start(out=planes[last][PACK - 1][:, : T // 2], in_=x_rows[last, PACK - 1][:, : T // 2])
+        nc.sync.dma_start(out=planes[last][PACK - 1][:, :CUT], in_=x_rows[last, PACK - 1][:, :CUT])
         for q in range(4):
             nc.sync.dma_start(
                 out=w_scale[32 * q : 32 * q + 4 * PASSES, :].bitcast(I32),
                 in_=w_scales[:, 4 * q : 4 * q + 4, :].bitcast(I32),
             )
-        nc.sync.dma_start(out=planes[last][PACK - 1][:, T // 2 :], in_=x_rows[last, PACK - 1][:, T // 2 :])
+        nc.sync.dma_start(out=planes[last][PACK - 1][:, CUT:], in_=x_rows[last, PACK - 1][:, CUT:])
         for a in range(PASSES):
             load_codes(a)
         with nc.allow_non_contiguous_dma(reason="one bias value a partition and output tile"):
@@ -86,7 +87,7 @@ def tile_picked_pick_lin_relu_sub_e_kernel(tc, xT, w_words, w_scales, b, offs, o
             (s, m): psum.tile([P, SLICE], F32, name=f"acc{s}_{m}") for s in range(SLICES) for m in range(M_TILES)
         }
         wide_codes = {}
-        result = [keep.tile([P, S], F32, name=f"result{m}") for m in range(M_TILES)]
+        result = keep.tile([P, M_TILES, S], F32, name="result")
         direct = SLICES - 1
 
         def span(s0, s1):
@@ -137,12 +138,12 @@ def tile_picked_pick_lin_relu_sub_e_kernel(tc, xT, w_words, w_scales, b, offs, o
                 )
 
         def finish(s):
-            nc.scalar.activation(result[0][:, span(s, s + 1)], acc[s, 0][:], RELU, bias=bias[:, 0:1])
-            nc.vector.tensor_scalar(result[1][:, span(s, s + 1)], acc[s, 1][:], bias[:, 1:2], 0.0, ADD, MAX)
+            nc.scalar.activation(result[:, 0, span(s, s + 1)], acc[s, 0][:], RELU, bias=bias[:, 0:1])
+            nc.vector.tensor_scalar(result[:, 1, span(s, s + 1)], acc[s, 1][:], bias[:, 1:2], 0.0, ADD, MAX)
 
         def store(s0, s1):
-            for m in range(M_TILES):
-                nc.sync.dma_start(out=out[m * P : (m + 1) * P, span(s0, s1)], in_=result[m][:, span(s0, s1)])
+            rows = out.rearrange("(m p) n -> p m n", p=P)
+            nc.sync.dma_start(out=rows[:, :, span(s0, s1)], in_=result[:, :, span(s0, s1)])
 
         for a in range(PASSES):
             gather(a, 0, 0, SLICES)

@@ -25,6 +25,7 @@ SLICES = S // SLICE
 M_TILES = N // P
 PER_COL = 16
 CUT = 640
+GROUPS = [(0, 256), (256, 384), (384, 512), (512, 768)]
 
 
 def tile_picked_pick_lin_relu_sub_e_kernel(tc, xT, w_words, w_scales, b, offs, out):
@@ -38,7 +39,9 @@ def tile_picked_pick_lin_relu_sub_e_kernel(tc, xT, w_words, w_scales, b, offs, o
         planes = [
             [keep.tile([P, T], F32, name=f"plane{a}_{t}", align_bytes=64) for t in range(PACK)] for a in range(PASSES)
         ]
-        w_codes = [keep.tile([P, N], U32, name=f"w_codes{a}", align_bytes=64) for a in range(PASSES)]
+        w_first = keep.tile([P, N], U32, name="w_first", align_bytes=64)
+        w_rest = keep.tile([P, PASSES - 1, N], U32, name="w_rest", align_bytes=64)
+        w_codes = [w_first[:]] + [w_rest[:, a, :] for a in range(PASSES - 1)]
         w_scale = keep.tile([P, N], U8, name="w_scale", align_bytes=64)
         bias = keep.tile([P, M_TILES], F32, name="bias")
         warm = keep.tile([P, 8], F32, name="warm")
@@ -49,11 +52,10 @@ def tile_picked_pick_lin_relu_sub_e_kernel(tc, xT, w_words, w_scales, b, offs, o
         def load_plane(a, t):
             nc.sync.dma_start(out=planes[a][t][:], in_=x_rows[a, t])
 
-        def load_codes(a):
-            nc.sync.dma_start(
-                out=w_codes[a][:].bitcast(I32),
-                in_=w_words[a].rearrange("p m r -> p (m r)").bitcast(I32),
-            )
+        w_rows = w_words.rearrange("a p m r -> p a (m r)").bitcast(I32)
+
+        def load_first_codes(cols):
+            nc.sync.dma_start(out=w_first[:, cols].bitcast(I32), in_=w_rows[:, 0, cols])
 
         nc.vector.memset(w_scale[:].bitcast(I32), 0)
         nc.vector.memset(warm[:], 0.0)
@@ -66,124 +68,127 @@ def tile_picked_pick_lin_relu_sub_e_kernel(tc, xT, w_words, w_scales, b, offs, o
                 if (a, t) not in ((0, 0), (last, PACK - 1)):
                     load_plane(a, t)
         nc.sync.dma_start(out=planes[last][PACK - 1][:, :CUT], in_=x_rows[last, PACK - 1][:, :CUT])
+        load_first_codes(slice(0, P))
+        nc.sync.dma_start(out=planes[last][PACK - 1][:, CUT:], in_=x_rows[last, PACK - 1][:, CUT:])
         for q in range(4):
             nc.sync.dma_start(
                 out=w_scale[32 * q : 32 * q + 4 * PASSES, :].bitcast(I32),
                 in_=w_scales[:, 4 * q : 4 * q + 4, :].bitcast(I32),
             )
-        nc.sync.dma_start(out=planes[last][PACK - 1][:, CUT:], in_=x_rows[last, PACK - 1][:, CUT:])
-        for a in range(PASSES):
-            load_codes(a)
+        load_first_codes(slice(P, N))
+        nc.sync.dma_start(out=w_rest[:].bitcast(I32), in_=w_rows[:, 1:, :])
         with nc.allow_non_contiguous_dma(reason="one bias value a partition and output tile"):
             nc.sync.dma_start(out=bias[:], in_=b.rearrange("(c p) o -> p (c o)", p=P))
 
         low = [keep.tile([P, 2, S], F32, name=f"low{a}") for a in range(PASSES)]
-        high_head = [keep.tile([P, 2, SLICE], F32, name=f"high_head{a}", align_bytes=64) for a in range(PASSES)]
-        high_rest = [keep.tile([P, 2, S - SLICE], F32, name=f"high_rest{a}") for a in range(PASSES)]
+        high = [keep.tile([P, 2, S], F32, name=f"high{a}") for a in range(last)]
+        high_head = keep.tile([P, 2, SLICE], F32, name="high_head", align_bytes=64)
+        high_rest = keep.tile([P, 2, SLICE], F32, name="high_rest")
         grouped = [keep.tile([P, S, PACK], BF16, name=f"grouped{a}", align_bytes=64) for a in range(PASSES)]
         x_scale = [keep.tile([P, S], U8, name=f"x_scale{a}", align_bytes=64) for a in range(PASSES)]
         x_codes = {}
-        acc = {
-            (s, m): psum.tile([P, SLICE], F32, name=f"acc{s}_{m}") for s in range(SLICES) for m in range(M_TILES)
-        }
-        wide_codes = {}
+        acc = {(g, m): psum.tile([P, 512], F32, name=f"acc{g}_{m}") for g in range(len(GROUPS)) for m in range(M_TILES)}
         result = keep.tile([P, M_TILES, S], F32, name="result")
-        direct = SLICES - 1
 
-        def span(s0, s1):
-            return slice(s0 * SLICE, s1 * SLICE)
+        def entries(lo, hi):
+            return offsets[:, lo // PER_COL : hi // PER_COL]
 
-        def picked(a, u, s0, s1):
+        def picked(a, u, lo, hi):
             if u == 0:
-                return low[a][:, :, span(s0, s1)]
-            if s0 == 0:
-                return high_head[a][:]
-            return high_rest[a][:, :, span(s0 - 1, s1 - 1)]
+                return low[a][:, :, lo:hi]
+            if a < last:
+                return high[a][:, :, lo:hi]
+            if hi <= SLICE:
+                return high_head[:, :, lo:hi]
+            return high_rest[:, :, lo - SLICE : hi - SLICE]
 
-        def window(a, t, s0, s1):
-            return planes[a][t][:].indirect(offsets[:, s0 * SLICE // PER_COL : s1 * SLICE // PER_COL])
+        def gather(a, t, lo, hi):
+            nc.vector.tensor_copy(picked(a, t // 2, lo, hi)[:, t % 2, :], planes[a][t][:].indirect(entries(lo, hi)))
 
-        def gather(a, t, s0, s1):
-            nc.vector.tensor_copy(picked(a, t // 2, s0, s1)[:, t % 2, :], window(a, t, s0, s1))
+        def interleave(a, u, lo, hi):
+            src = picked(a, u, lo, hi).rearrange("p t n -> p n t")
+            nc.scalar.activation(grouped[a][:, lo:hi, 2 * u : 2 * u + 2], src, COPY)
 
-        def interleave(a, u, s0, s1):
-            src = picked(a, u, s0, s1).rearrange("p t n -> p n t")
-            nc.scalar.activation(grouped[a][:, span(s0, s1), 2 * u : 2 * u + 2], src, COPY)
-
-        def quantize(a, s0, s1, tag):
-            codes = keep.tile([P, (s1 - s0) * SLICE], U32, name=f"x_codes{a}_{s0}", tag=tag, align_bytes=64)
-            wide_codes[a, s0] = codes
-            for s in range(s0, s1):
-                x_codes[a, s] = codes[:, span(s - s0, s - s0 + 1)]
+        def quantize(a, lo, hi, tag):
+            codes = keep.tile([P, hi - lo], U32, name=f"x_codes{a}_{lo}", tag=tag, align_bytes=64)
+            x_codes[a, lo] = codes
             nc.vector.quantize_mx(
                 out=codes[:].bitcast(FP8X4),
-                scales=x_scale[a][:, span(s0, s1)],
-                in_=grouped[a][:, span(s0, s1), :].rearrange("p n t -> p (n t)"),
+                scales=x_scale[a][:, lo:hi],
+                in_=grouped[a][:, lo:hi, :].rearrange("p n t -> p (n t)"),
             )
 
-        def gather_grouped(a, t, s):
-            nc.vector.tensor_copy(grouped[a][:, span(s, s + 1), t], window(a, t, s, s + 1))
+        def codes_of(a, lo, hi):
+            start = max(s for (aa, s) in x_codes if aa == a and s <= lo)
+            return x_codes[a, start][:, lo - start : hi - start]
 
-        def multiply(a, s):
+        def gather_grouped(a, t, lo, hi):
+            nc.vector.tensor_copy(grouped[a][:, lo:hi, t], planes[a][t][:].indirect(entries(lo, hi)))
+
+        def multiply(a, g):
+            lo, hi = GROUPS[g]
             for m in range(M_TILES):
                 cols = slice(m * P, (m + 1) * P)
                 nc.tensor.matmul_mx(
-                    out=acc[s, m][:],
+                    out=acc[g, m][:, : hi - lo],
                     lhsT=w_codes[a][:, cols].bitcast(FP8X4),
                     lhsT_scale=w_scale[4 * a : P, cols],
-                    rhs=x_codes[a, s].bitcast(FP8X4),
-                    rhs_scale=x_scale[a][:, span(s, s + 1)],
+                    rhs=codes_of(a, lo, hi).bitcast(FP8X4),
+                    rhs_scale=x_scale[a][:, lo:hi],
                     start=(a == 0),
                     stop=(a == last),
                 )
 
-        def finish(s):
-            nc.scalar.activation(result[:, 0, span(s, s + 1)], acc[s, 0][:], RELU, bias=bias[:, 0:1])
-            nc.vector.tensor_scalar(result[:, 1, span(s, s + 1)], acc[s, 1][:], bias[:, 1:2], 0.0, ADD, MAX)
+        def finish(g):
+            lo, hi = GROUPS[g]
+            nc.scalar.activation(result[:, 0, lo:hi], acc[g, 0][:, : hi - lo], RELU, bias=bias[:, 0:1])
+            nc.vector.tensor_scalar(result[:, 1, lo:hi], acc[g, 1][:, : hi - lo], bias[:, 1:2], 0.0, ADD, MAX)
 
-        def store(s0, s1):
+        def store(lo, hi):
             rows = out.rearrange("(m p) n -> p m n", p=P)
-            nc.sync.dma_start(out=rows[:, :, span(s0, s1)], in_=result[:, :, span(s0, s1)])
+            nc.sync.dma_start(out=rows[:, :, lo:hi], in_=result[:, :, lo:hi])
 
+        thirds = [(s * SLICE, (s + 1) * SLICE) for s in range(SLICES)]
         for a in range(PASSES):
-            gather(a, 0, 0, SLICES)
+            gather(a, 0, 0, S)
             if a > 0:
-                quantize(a - 1, 1, SLICES, f"plane{a}_0")
-            gather(a, 1, 0, SLICES)
-            interleave(a, 0, 0, SLICES)
-            gather(a, 2, 0, 1)
+                quantize(a - 1, SLICE, S, f"plane{a}_0")
+            gather(a, 1, 0, S)
+            interleave(a, 0, 0, S)
             if a < last:
-                gather(a, 2, 1, SLICES)
-                for s in range(SLICES):
-                    gather(a, 3, s, s + 1)
-                    interleave(a, 1, s, s + 1)
-                quantize(a, 0, 1, f"x_codes{a}_0")
+                gather(a, 2, 0, S)
+                for lo, hi in thirds:
+                    gather(a, 3, lo, hi)
+                    interleave(a, 1, lo, hi)
+                quantize(a, 0, SLICE, f"x_codes{a}_0")
 
-        gather(last, 2, 1, direct)
-        gather_grouped(last, 2, direct)
-        for s in range(direct):
-            gather(last, 3, s, s + 1)
-            interleave(last, 1, s, s + 1)
-        gather_grouped(last, 3, direct)
-        quantize(last, 0, 1, "x_codes_first")
-        quantize(last, 2, 3, f"high_head{last}")
-        quantize(last, 1, 2, "x_codes_last")
-        for i in range(2):
-            spare = psum.tile([P, 2 * SLICE], F32, name=f"spare{i}")
+        for lo, hi in thirds[:2]:
+            gather(last, 2, lo, hi)
+        gather_grouped(last, 2, *GROUPS[3])
+        for lo, hi in thirds[:2]:
+            gather(last, 3, lo, hi)
+        for lo, hi in GROUPS[:3]:
+            interleave(last, 1, lo, hi)
+        gather_grouped(last, 3, *GROUPS[3])
+        quantize(last, *GROUPS[0], "x_codes_first")
+        quantize(last, *GROUPS[3], "high_head")
+        quantize(last, *GROUPS[1], "x_codes_third")
+        quantize(last, *GROUPS[2], "x_codes_last")
+        for m in range(M_TILES):
             nc.tensor.matmul_mx(
-                out=spare[:],
-                lhsT=x_codes[0, 0][:, 0:P].bitcast(FP8X4),
-                lhsT_scale=w_scale[:, 0:P],
-                rhs=wide_codes[0, 1][:].bitcast(FP8X4),
-                rhs_scale=x_scale[0][:, span(1, SLICES)],
+                out=acc[2, m][:],
+                lhsT=w_codes[0][:, 0:P].bitcast(FP8X4),
+                lhsT_scale=x_scale[0][:, 0:P],
+                rhs=codes_of(0, SLICE, S).bitcast(FP8X4),
+                rhs_scale=x_scale[0][:, SLICE:S],
                 start=True,
                 stop=True,
             )
-        order = [0, 2, 1]
+        order = [0, 3, 1, 2]
         for a in range(PASSES):
-            for s in order:
-                multiply(a, s)
-        for s in order:
-            finish(s)
-        store(0, 1)
-        store(1, SLICES)
+            for g in order:
+                multiply(a, g)
+        for g in order:
+            finish(g)
+        store(0, SLICE)
+        store(SLICE, S)

@@ -24,7 +24,6 @@ SLICE = 256
 SLICES = S // SLICE
 M_TILES = N // P
 PER_COL = 16
-CUT = 640
 GROUPS = [(0, 256), (256, 384), (384, 512), (512, 768)]
 
 
@@ -42,7 +41,7 @@ def tile_picked_pick_lin_relu_sub_e_kernel(tc, xT, w_words, w_scales, b, offs, o
         w_first = keep.tile([P, N], U32, name="w_first", align_bytes=64)
         w_rest = keep.tile([P, PASSES - 1, N], U32, name="w_rest", align_bytes=64)
         w_codes = [w_first[:]] + [w_rest[:, a, :] for a in range(PASSES - 1)]
-        w_scale = keep.tile([P, N], U8, name="w_scale", align_bytes=64)
+        w_scale = keep.tile([P, PASSES, N], U8, name="w_scale", align_bytes=64)
         bias = keep.tile([P, M_TILES], F32, name="bias")
         warm = keep.tile([P, 8], F32, name="warm")
         warm_out = keep.tile([P, 8], F32, name="warm_out")
@@ -63,18 +62,15 @@ def tile_picked_pick_lin_relu_sub_e_kernel(tc, xT, w_words, w_scales, b, offs, o
         load_plane(0, 0)
         nc.sync.dma_start(offsets[:], offs)
         nc.scalar.activation(warm_out[:], warm[:], RELU)
+        load_plane(0, 1)
+        scale_rows = w_scales.rearrange("a (q r) m -> r q a m", r=4).bitcast(I32)
+        for r in range(4):
+            nc.sync.dma_start(out=w_scale[r:P:32].bitcast(I32), in_=scale_rows[r])
         for a in range(PASSES):
             for t in range(PACK):
-                if (a, t) not in ((0, 0), (last, PACK - 1)):
+                if (a, t) > (0, 1):
                     load_plane(a, t)
-        nc.sync.dma_start(out=planes[last][PACK - 1][:, :CUT], in_=x_rows[last, PACK - 1][:, :CUT])
         load_first_codes(slice(0, P))
-        nc.sync.dma_start(out=planes[last][PACK - 1][:, CUT:], in_=x_rows[last, PACK - 1][:, CUT:])
-        for q in range(4):
-            nc.sync.dma_start(
-                out=w_scale[32 * q : 32 * q + 4 * PASSES, :].bitcast(I32),
-                in_=w_scales[:, 4 * q : 4 * q + 4, :].bitcast(I32),
-            )
         load_first_codes(slice(P, N))
         nc.sync.dma_start(out=w_rest[:].bitcast(I32), in_=w_rows[:, 1:, :])
         with nc.allow_non_contiguous_dma(reason="one bias value a partition and output tile"):
@@ -132,7 +128,7 @@ def tile_picked_pick_lin_relu_sub_e_kernel(tc, xT, w_words, w_scales, b, offs, o
                 nc.tensor.matmul_mx(
                     out=acc[g, m][:, : hi - lo],
                     lhsT=w_codes[a][:, cols].bitcast(FP8X4),
-                    lhsT_scale=w_scale[4 * a : P, cols],
+                    lhsT_scale=w_scale[:, a, cols],
                     rhs=codes_of(a, lo, hi).bitcast(FP8X4),
                     rhs_scale=x_scale[a][:, lo:hi],
                     start=(a == 0),
@@ -151,9 +147,11 @@ def tile_picked_pick_lin_relu_sub_e_kernel(tc, xT, w_words, w_scales, b, offs, o
         thirds = [(s * SLICE, (s + 1) * SLICE) for s in range(SLICES)]
         for a in range(PASSES):
             gather(a, 0, 0, S)
-            if a > 0:
+            if 0 < a < last:
                 quantize(a - 1, SLICE, S, f"plane{a}_0")
             gather(a, 1, 0, S)
+            if a == last:
+                quantize(a - 1, SLICE, S, f"plane{a}_1")
             interleave(a, 0, 0, S)
             if a < last:
                 gather(a, 2, 0, S)
@@ -177,10 +175,10 @@ def tile_picked_pick_lin_relu_sub_e_kernel(tc, xT, w_words, w_scales, b, offs, o
         for m in range(M_TILES):
             nc.tensor.matmul_mx(
                 out=acc[2, m][:],
-                lhsT=w_codes[0][:, 0:P].bitcast(FP8X4),
+                lhsT=codes_of(0, 0, P).bitcast(FP8X4),
                 lhsT_scale=x_scale[0][:, 0:P],
-                rhs=codes_of(0, SLICE, S).bitcast(FP8X4),
-                rhs_scale=x_scale[0][:, SLICE:S],
+                rhs=codes_of(last - 1, SLICE, S).bitcast(FP8X4),
+                rhs_scale=x_scale[last - 1][:, SLICE:S],
                 start=True,
                 stop=True,
             )

@@ -76,7 +76,7 @@ def tile_picked_pick_lin_relu_sub_e_kernel(tc, xT, w_words, w_scales, b, offs, o
         with nc.allow_non_contiguous_dma(reason="one bias value a partition and output tile"):
             nc.sync.dma_start(out=bias[:], in_=b.rearrange("(c p) o -> p (c o)", p=P))
 
-        low = [keep.tile([P, 2, S], F32, name=f"low{a}") for a in range(PASSES)]
+        low = [keep.tile([P, 2, S], BF16 if a > 0 else F32, name=f"low{a}", align_bytes=64) for a in range(PASSES)]
         high = [keep.tile([P, 2, S], F32, name=f"high{a}") for a in range(last)]
         high_head = keep.tile([P, 2, SLICE], F32, name="high_head", align_bytes=64)
         high_rest = keep.tile([P, 2, SLICE], F32, name="high_rest")
@@ -105,11 +105,14 @@ def tile_picked_pick_lin_relu_sub_e_kernel(tc, xT, w_words, w_scales, b, offs, o
             src = picked(a, u, lo, hi).rearrange("p t n -> p n t")
             nc.scalar.activation(grouped[a][:, lo:hi, 2 * u : 2 * u + 2], src, COPY)
 
-        def quantize(a, lo, hi, tag):
-            codes = keep.tile([P, hi - lo], U32, name=f"x_codes{a}_{lo}", tag=tag, align_bytes=64)
-            x_codes[a, lo] = codes
+        def new_codes(a, lo, hi, tag):
+            x_codes[a, lo] = keep.tile([P, hi - lo], U32, name=f"x_codes{a}_{lo}", tag=tag, align_bytes=64)
+
+        def quantize(a, lo, hi, tag=None):
+            if tag is not None:
+                new_codes(a, lo, hi, tag)
             nc.vector.quantize_mx(
-                out=codes[:].bitcast(FP8X4),
+                out=codes_of(a, lo, hi).bitcast(FP8X4),
                 scales=x_scale[a][:, lo:hi],
                 in_=grouped[a][:, lo:hi, :].rearrange("p n t -> p (n t)"),
             )
@@ -145,13 +148,25 @@ def tile_picked_pick_lin_relu_sub_e_kernel(tc, xT, w_words, w_scales, b, offs, o
             nc.sync.dma_start(out=rows[:, :, lo:hi], in_=result[:, :, lo:hi])
 
         thirds = [(s * SLICE, (s + 1) * SLICE) for s in range(SLICES)]
+        def gather_first(a):
+            rounded = keep.tile([P, T], BF16, name=f"rounded{a}", align_bytes=64)
+            nc.vector.tensor_copy(rounded[:], planes[a][0][:])
+            nc.scalar.activation(low[a][:, 0, :], rounded[:].indirect(entries(0, S)), COPY)
+
         for a in range(PASSES):
-            gather(a, 0, 0, S)
+            if a == 0:
+                gather(a, 0, 0, S)
+            else:
+                gather_first(a)
             if 0 < a < last:
                 quantize(a - 1, SLICE, S, f"plane{a}_0")
+            if a == last:
+                quantize(a - 1, *GROUPS[1], f"plane{a}_0")
             gather(a, 1, 0, S)
             if a == last:
-                quantize(a - 1, SLICE, S, f"plane{a}_1")
+                new_codes(a - 1, GROUPS[2][0], S, f"plane{a}_1")
+                quantize(a - 1, *GROUPS[2])
+                quantize(a - 1, *GROUPS[3])
             interleave(a, 0, 0, S)
             if a < last:
                 gather(a, 2, 0, S)
@@ -175,10 +190,10 @@ def tile_picked_pick_lin_relu_sub_e_kernel(tc, xT, w_words, w_scales, b, offs, o
         for m in range(M_TILES):
             nc.tensor.matmul_mx(
                 out=acc[2, m][:],
-                lhsT=codes_of(0, 0, P).bitcast(FP8X4),
-                lhsT_scale=x_scale[0][:, 0:P],
-                rhs=codes_of(last - 1, SLICE, S).bitcast(FP8X4),
-                rhs_scale=x_scale[last - 1][:, SLICE:S],
+                lhsT=codes_of(last - 1, S - P, S).bitcast(FP8X4),
+                lhsT_scale=x_scale[last - 1][:, S - P : S],
+                rhs=codes_of(0, SLICE, S).bitcast(FP8X4),
+                rhs_scale=x_scale[0][:, SLICE:S],
                 start=True,
                 stop=True,
             )

@@ -20,11 +20,14 @@ MAX = mybir.AluOpType.max
 P = 128
 PACK = 4
 PASSES = K // (P * PACK)
-SLICE = 256
-SLICES = S // SLICE
+THIRD = S // 3
 M_TILES = N // P
 PER_COL = 16
-GROUPS = [(0, 256), (256, 384), (384, 512), (512, 768)]
+QUADRANT = 32
+SCALE_ROWS = 4
+BANK = 512
+GROUPS = [(0, THIRD), (THIRD, THIRD + P), (THIRD + P, 2 * THIRD), (2 * THIRD, S)]
+FINISH_ORDER = [0, 3, 1, 2]
 
 
 def tile_picked_pick_lin_relu_sub_e_kernel(tc, xT, w_words, w_scales, b, offs, out):
@@ -43,8 +46,6 @@ def tile_picked_pick_lin_relu_sub_e_kernel(tc, xT, w_words, w_scales, b, offs, o
         w_codes = [w_first[:]] + [w_rest[:, a, :] for a in range(PASSES - 1)]
         w_scale = keep.tile([P, PASSES, N], U8, name="w_scale", align_bytes=64)
         bias = keep.tile([P, M_TILES], F32, name="bias")
-        warm = keep.tile([P, 8], F32, name="warm")
-        warm_out = keep.tile([P, 8], F32, name="warm_out")
 
         x_rows = xT.rearrange("(a p t) n -> a t p n", p=P, t=PACK)
 
@@ -57,15 +58,13 @@ def tile_picked_pick_lin_relu_sub_e_kernel(tc, xT, w_words, w_scales, b, offs, o
             nc.sync.dma_start(out=w_first[:, cols].bitcast(I32), in_=w_rows[:, 0, cols])
 
         nc.vector.memset(w_scale[:].bitcast(I32), 0)
-        nc.vector.memset(warm[:], 0.0)
 
         load_plane(0, 0)
         nc.sync.dma_start(offsets[:], offs)
-        nc.scalar.activation(warm_out[:], warm[:], RELU)
         load_plane(0, 1)
-        scale_rows = w_scales.rearrange("a (q r) m -> r q a m", r=4).bitcast(I32)
-        for r in range(4):
-            nc.sync.dma_start(out=w_scale[r:P:32].bitcast(I32), in_=scale_rows[r])
+        scale_rows = w_scales.rearrange("a (q r) m -> r q a m", r=SCALE_ROWS).bitcast(I32)
+        for r in range(SCALE_ROWS):
+            nc.sync.dma_start(out=w_scale[r:P:QUADRANT].bitcast(I32), in_=scale_rows[r])
         for a in range(PASSES):
             for t in range(PACK):
                 if (a, t) > (0, 1):
@@ -78,51 +77,58 @@ def tile_picked_pick_lin_relu_sub_e_kernel(tc, xT, w_words, w_scales, b, offs, o
 
         low = [keep.tile([P, 2, S], BF16 if a > 0 else F32, name=f"low{a}", align_bytes=64) for a in range(PASSES)]
         high = [keep.tile([P, 2, S], F32, name=f"high{a}") for a in range(last)]
-        high_head = keep.tile([P, 2, SLICE], F32, name="high_head", align_bytes=64)
-        high_rest = keep.tile([P, 2, SLICE], F32, name="high_rest")
+        high_head = keep.tile([P, 2, THIRD], F32, name="high_head", align_bytes=64)
+        high_rest = keep.tile([P, 2, THIRD], F32, name="high_rest")
         grouped = [keep.tile([P, S, PACK], BF16, name=f"grouped{a}", align_bytes=64) for a in range(PASSES)]
         x_scale = [keep.tile([P, S], U8, name=f"x_scale{a}", align_bytes=64) for a in range(PASSES)]
         x_codes = {}
-        acc = {(g, m): psum.tile([P, 512], F32, name=f"acc{g}_{m}") for g in range(len(GROUPS)) for m in range(M_TILES)}
+        acc = {(g, m): psum.tile([P, BANK], F32, name=f"acc{g}_{m}") for g in range(len(GROUPS)) for m in range(M_TILES)}
         result = keep.tile([P, M_TILES, S], F32, name="result")
 
         def entries(lo, hi):
             return offsets[:, lo // PER_COL : hi // PER_COL]
 
-        def picked(a, u, lo, hi):
-            if u == 0:
+        def picked(a, pair, lo, hi):
+            if pair == 0:
                 return low[a][:, :, lo:hi]
             if a < last:
                 return high[a][:, :, lo:hi]
-            if hi <= SLICE:
+            if hi <= THIRD:
                 return high_head[:, :, lo:hi]
-            return high_rest[:, :, lo - SLICE : hi - SLICE]
+            return high_rest[:, :, lo - THIRD : hi - THIRD]
 
         def gather(a, t, lo, hi):
             nc.vector.tensor_copy(picked(a, t // 2, lo, hi)[:, t % 2, :], planes[a][t][:].indirect(entries(lo, hi)))
 
-        def interleave(a, u, lo, hi):
-            src = picked(a, u, lo, hi).rearrange("p t n -> p n t")
-            nc.scalar.activation(grouped[a][:, lo:hi, 2 * u : 2 * u + 2], src, COPY)
+        def gather_on_scalar(a):
+            rounded = keep.tile([P, T], BF16, name=f"rounded{a}", align_bytes=64)
+            nc.vector.tensor_copy(rounded[:], planes[a][0][:])
+            nc.scalar.activation(low[a][:, 0, :], rounded[:].indirect(entries(0, S)), COPY)
+
+        def gather_grouped(a, t, lo, hi):
+            nc.vector.tensor_copy(grouped[a][:, lo:hi, t], planes[a][t][:].indirect(entries(lo, hi)))
+
+        def interleave(a, pair, lo, hi):
+            src = picked(a, pair, lo, hi).rearrange("p t n -> p n t")
+            nc.scalar.activation(grouped[a][:, lo:hi, 2 * pair : 2 * pair + 2], src, COPY)
 
         def new_codes(a, lo, hi, tag):
             x_codes[a, lo] = keep.tile([P, hi - lo], U32, name=f"x_codes{a}_{lo}", tag=tag, align_bytes=64)
 
-        def quantize(a, lo, hi, tag=None):
-            if tag is not None:
-                new_codes(a, lo, hi, tag)
+        def codes_of(a, lo, hi):
+            start = max(first for (owner, first) in x_codes if owner == a and first <= lo)
+            return x_codes[a, start][:, lo - start : hi - start]
+
+        def quantize(a, lo, hi):
             nc.vector.quantize_mx(
                 out=codes_of(a, lo, hi).bitcast(FP8X4),
                 scales=x_scale[a][:, lo:hi],
                 in_=grouped[a][:, lo:hi, :].rearrange("p n t -> p (n t)"),
             )
 
-        def codes_of(a, lo, hi):
-            start = max(s for (aa, s) in x_codes if aa == a and s <= lo)
-            return x_codes[a, start][:, lo - start : hi - start]
-
-        def gather_grouped(a, t, lo, hi):
-            nc.vector.tensor_copy(grouped[a][:, lo:hi, t], planes[a][t][:].indirect(entries(lo, hi)))
+        def quantize_into(a, lo, hi, tag):
+            new_codes(a, lo, hi, tag)
+            quantize(a, lo, hi)
 
         def multiply(a, g):
             lo, hi = GROUPS[g]
@@ -147,21 +153,17 @@ def tile_picked_pick_lin_relu_sub_e_kernel(tc, xT, w_words, w_scales, b, offs, o
             rows = out.rearrange("(m p) n -> p m n", p=P)
             nc.sync.dma_start(out=rows[:, :, lo:hi], in_=result[:, :, lo:hi])
 
-        thirds = [(s * SLICE, (s + 1) * SLICE) for s in range(SLICES)]
-        def gather_first(a):
-            rounded = keep.tile([P, T], BF16, name=f"rounded{a}", align_bytes=64)
-            nc.vector.tensor_copy(rounded[:], planes[a][0][:])
-            nc.scalar.activation(low[a][:, 0, :], rounded[:].indirect(entries(0, S)), COPY)
+        thirds = [(lo, lo + THIRD) for lo in range(0, S, THIRD)]
 
         for a in range(PASSES):
             if a == 0:
                 gather(a, 0, 0, S)
             else:
-                gather_first(a)
+                gather_on_scalar(a)
             if 0 < a < last:
-                quantize(a - 1, SLICE, S, f"plane{a}_0")
+                quantize_into(a - 1, THIRD, S, f"plane{a}_0")
             if a == last:
-                quantize(a - 1, *GROUPS[1], f"plane{a}_0")
+                quantize_into(a - 1, *GROUPS[1], f"plane{a}_0")
             gather(a, 1, 0, S)
             if a == last:
                 new_codes(a - 1, GROUPS[2][0], S, f"plane{a}_1")
@@ -173,7 +175,7 @@ def tile_picked_pick_lin_relu_sub_e_kernel(tc, xT, w_words, w_scales, b, offs, o
                 for lo, hi in thirds:
                     gather(a, 3, lo, hi)
                     interleave(a, 1, lo, hi)
-                quantize(a, 0, SLICE, f"x_codes{a}_0")
+                quantize_into(a, 0, THIRD, f"x_codes{a}_0")
 
         for lo, hi in thirds[:2]:
             gather(last, 2, lo, hi)
@@ -183,25 +185,25 @@ def tile_picked_pick_lin_relu_sub_e_kernel(tc, xT, w_words, w_scales, b, offs, o
         for lo, hi in GROUPS[:3]:
             interleave(last, 1, lo, hi)
         gather_grouped(last, 3, *GROUPS[3])
-        quantize(last, *GROUPS[0], "x_codes_first")
-        quantize(last, *GROUPS[3], "high_head")
-        quantize(last, *GROUPS[1], "x_codes_third")
-        quantize(last, *GROUPS[2], "x_codes_last")
+        quantize_into(last, *GROUPS[0], "x_codes_first")
+        quantize_into(last, *GROUPS[3], "high_head")
+        quantize_into(last, *GROUPS[1], "x_codes_third")
+        quantize_into(last, *GROUPS[2], "x_codes_last")
+
         for m in range(M_TILES):
             nc.tensor.matmul_mx(
                 out=acc[2, m][:],
                 lhsT=codes_of(last - 1, S - P, S).bitcast(FP8X4),
                 lhsT_scale=x_scale[last - 1][:, S - P : S],
-                rhs=codes_of(0, SLICE, S).bitcast(FP8X4),
-                rhs_scale=x_scale[0][:, SLICE:S],
+                rhs=codes_of(0, THIRD, S).bitcast(FP8X4),
+                rhs_scale=x_scale[0][:, THIRD:S],
                 start=True,
                 stop=True,
             )
-        order = [0, 3, 1, 2]
         for a in range(PASSES):
-            for g in order:
+            for g in FINISH_ORDER:
                 multiply(a, g)
-        for g in order:
+        for g in FINISH_ORDER:
             finish(g)
-        store(0, SLICE)
-        store(SLICE, S)
+        store(0, THIRD)
+        store(THIRD, S)

@@ -190,16 +190,6 @@ def tile_picked_pick_lin_relu_sub_e_kernel(tc, xT, w_words, w_scales, b, offs, o
         quantize_into(last, *GROUPS[1], "x_codes_third")
         quantize_into(last, *GROUPS[2], "x_codes_last")
 
-        for m in range(M_TILES):
-            nc.tensor.matmul_mx(
-                out=acc[2, m][:],
-                lhsT=codes_of(last - 1, S - P, S).bitcast(FP8X4),
-                lhsT_scale=x_scale[last - 1][:, S - P : S],
-                rhs=codes_of(0, THIRD, S).bitcast(FP8X4),
-                rhs_scale=x_scale[0][:, THIRD:S],
-                start=True,
-                stop=True,
-            )
         for a in range(PASSES):
             for g in FINISH_ORDER:
                 multiply(a, g)

@@ -26,8 +26,7 @@ PER_COL = 16
 QUADRANT = 32
 SCALE_ROWS = 4
 BANK = 512
-GROUPS = [(0, THIRD), (THIRD, THIRD + P), (THIRD + P, 2 * THIRD), (2 * THIRD, S)]
-FINISH_ORDER = [0, 3, 1, 2]
+LOADS = [(0, 0, 2), (0, 2, 2), (1, 0, 2), (1, 2, 2), (2, 0, 2), (2, 2, 1), (2, 3, 1)]
 
 
 def tile_picked_pick_lin_relu_sub_e_kernel(tc, xT, w_words, w_scales, b, offs, out):
@@ -38,162 +37,134 @@ def tile_picked_pick_lin_relu_sub_e_kernel(tc, xT, w_words, w_scales, b, offs, o
         psum = ctx.enter_context(tc.psum_pool(name="psum", bufs=1))
 
         offsets = keep.tile([P, S // PER_COL], U16, name="offsets")
-        planes = [
-            [keep.tile([P, T], F32, name=f"plane{a}_{t}", align_bytes=64) for t in range(PACK)] for a in range(PASSES)
-        ]
-        w_first = keep.tile([P, N], U32, name="w_first", align_bytes=64)
-        w_rest = keep.tile([P, PASSES - 1, N], U32, name="w_rest", align_bytes=64)
-        w_codes = [w_first[:]] + [w_rest[:, a, :] for a in range(PASSES - 1)]
+        w_codes = [keep.tile([P, N], U32, name=f"w_codes{a}", align_bytes=64) for a in range(PASSES)]
         w_scale = keep.tile([P, PASSES, N], U8, name="w_scale", align_bytes=64)
         bias = keep.tile([P, M_TILES], F32, name="bias")
 
-        x_rows = xT.rearrange("(a p t) n -> a t p n", p=P, t=PACK)
+        x_rows = xT.rearrange("(a p t) n -> a p (t n)", p=P, t=PACK)
+        w_rows = w_words.rearrange("a p m r -> a p (m r)").bitcast(I32)
+        plane = {}
 
-        def load_plane(a, t):
-            nc.sync.dma_start(out=planes[a][t][:], in_=x_rows[a, t])
+        def load_planes(a, t0, count):
+            tile = keep.tile([P, count * T], F32, name=f"planes{a}_{t0}", align_bytes=64)
+            nc.sync.dma_start(out=tile[:], in_=x_rows[a, :, t0 * T : (t0 + count) * T])
+            for t in range(count):
+                plane[a, t0 + t] = tile[:, t * T : (t + 1) * T]
 
-        w_rows = w_words.rearrange("a p m r -> p a (m r)").bitcast(I32)
-
-        def load_first_codes(cols):
-            nc.sync.dma_start(out=w_first[:, cols].bitcast(I32), in_=w_rows[:, 0, cols])
+        def load_codes(a):
+            nc.sync.dma_start(out=w_codes[a][:].bitcast(I32), in_=w_rows[a])
 
         nc.vector.memset(w_scale[:].bitcast(I32), 0)
 
-        load_plane(0, 0)
+        load_planes(*LOADS[0])
         nc.sync.dma_start(offsets[:], offs)
-        load_plane(0, 1)
+        load_planes(*LOADS[1])
         scale_rows = w_scales.rearrange("a (q r) m -> r q a m", r=SCALE_ROWS).bitcast(I32)
         for r in range(SCALE_ROWS):
             nc.sync.dma_start(out=w_scale[r:P:QUADRANT].bitcast(I32), in_=scale_rows[r])
-        for a in range(PASSES):
-            for t in range(PACK):
-                if (a, t) > (0, 1):
-                    load_plane(a, t)
-        load_first_codes(slice(0, P))
-        load_first_codes(slice(P, N))
-        nc.sync.dma_start(out=w_rest[:].bitcast(I32), in_=w_rows[:, 1:, :])
+        for load in LOADS[2:-1]:
+            load_planes(*load)
+        load_codes(0)
+        load_planes(*LOADS[-1])
+        load_codes(1)
+        load_codes(2)
         with nc.allow_non_contiguous_dma(reason="one bias value a partition and output tile"):
             nc.sync.dma_start(out=bias[:], in_=b.rearrange("(c p) o -> p (c o)", p=P))
 
-        low = [keep.tile([P, 2, S], BF16 if a > 0 else F32, name=f"low{a}", align_bytes=64) for a in range(PASSES)]
-        high = [keep.tile([P, 2, S], F32, name=f"high{a}") for a in range(last)]
-        high_head = keep.tile([P, 2, THIRD], F32, name="high_head", align_bytes=64)
-        high_rest = keep.tile([P, 2, THIRD], F32, name="high_rest")
-        grouped = [keep.tile([P, S, PACK], BF16, name=f"grouped{a}", align_bytes=64) for a in range(PASSES)]
-        x_scale = [keep.tile([P, S], U8, name=f"x_scale{a}", align_bytes=64) for a in range(PASSES)]
-        x_codes = {}
-        acc = {(g, m): psum.tile([P, BANK], F32, name=f"acc{g}_{m}") for g in range(len(GROUPS)) for m in range(M_TILES)}
-        result = keep.tile([P, M_TILES, S], F32, name="result")
+        thirds = range(3)
+        grouped = [[keep.tile([P, THIRD, PACK], BF16, name=f"grouped{a}_{g}", align_bytes=64) for g in thirds] for a in range(PASSES)]
+        x_codes = [[keep.tile([P, THIRD], U32, name=f"x_codes{a}_{g}", align_bytes=64) for g in thirds] for a in range(PASSES)]
+        x_scale = [[keep.tile([P, THIRD], U8, name=f"x_scale{a}_{g}", align_bytes=64) for g in thirds] for a in range(PASSES)]
+        acc = [[psum.tile([P, BANK], F32, name=f"acc{g}_{m}") for m in range(M_TILES)] for g in thirds]
+        result = [keep.tile([P, M_TILES, THIRD], F32, name=f"result{g}") for g in thirds]
 
-        def entries(lo, hi):
-            return offsets[:, lo // PER_COL : hi // PER_COL]
+        def window(a, t, lo, hi):
+            return plane[a, t].indirect(offsets[:, lo // PER_COL : hi // PER_COL])
 
-        def picked(a, pair, lo, hi):
-            if pair == 0:
-                return low[a][:, :, lo:hi]
-            if a < last:
-                return high[a][:, :, lo:hi]
-            if hi <= THIRD:
-                return high_head[:, :, lo:hi]
-            return high_rest[:, :, lo - THIRD : hi - THIRD]
+        def third(a, t, g):
+            return window(a, t, g * THIRD, (g + 1) * THIRD)
 
-        def gather(a, t, lo, hi):
-            nc.vector.tensor_copy(picked(a, t // 2, lo, hi)[:, t % 2, :], planes[a][t][:].indirect(entries(lo, hi)))
+        def on_vector(dst, src):
+            nc.vector.tensor_copy(dst, src)
 
-        def gather_on_scalar(a):
-            rounded = keep.tile([P, T], BF16, name=f"rounded{a}", align_bytes=64)
-            nc.vector.tensor_copy(rounded[:], planes[a][0][:])
-            nc.scalar.activation(low[a][:, 0, :], rounded[:].indirect(entries(0, S)), COPY)
+        def on_scalar(dst, src):
+            nc.scalar.activation(dst, src, COPY)
 
-        def gather_grouped(a, t, lo, hi):
-            nc.vector.tensor_copy(grouped[a][:, lo:hi, t], planes[a][t][:].indirect(entries(lo, hi)))
-
-        def interleave(a, pair, lo, hi):
-            src = picked(a, pair, lo, hi).rearrange("p t n -> p n t")
-            nc.scalar.activation(grouped[a][:, lo:hi, 2 * pair : 2 * pair + 2], src, COPY)
-
-        def new_codes(a, lo, hi, tag):
-            x_codes[a, lo] = keep.tile([P, hi - lo], U32, name=f"x_codes{a}_{lo}", tag=tag, align_bytes=64)
-
-        def codes_of(a, lo, hi):
-            start = max(first for (owner, first) in x_codes if owner == a and first <= lo)
-            return x_codes[a, start][:, lo - start : hi - start]
-
-        def quantize(a, lo, hi):
+        def quantize(a, g, lo, hi):
             nc.vector.quantize_mx(
-                out=codes_of(a, lo, hi).bitcast(FP8X4),
-                scales=x_scale[a][:, lo:hi],
-                in_=grouped[a][:, lo:hi, :].rearrange("p n t -> p (n t)"),
+                out=x_codes[a][g][:, lo:hi].bitcast(FP8X4),
+                scales=x_scale[a][g][:, lo:hi],
+                in_=grouped[a][g][:, lo:hi, :].rearrange("p n t -> p (n t)"),
             )
 
-        def quantize_into(a, lo, hi, tag):
-            new_codes(a, lo, hi, tag)
-            quantize(a, lo, hi)
-
         def multiply(a, g):
-            lo, hi = GROUPS[g]
             for m in range(M_TILES):
                 cols = slice(m * P, (m + 1) * P)
                 nc.tensor.matmul_mx(
-                    out=acc[g, m][:, : hi - lo],
+                    out=acc[g][m][:, :THIRD],
                     lhsT=w_codes[a][:, cols].bitcast(FP8X4),
                     lhsT_scale=w_scale[:, a, cols],
-                    rhs=codes_of(a, lo, hi).bitcast(FP8X4),
-                    rhs_scale=x_scale[a][:, lo:hi],
+                    rhs=x_codes[a][g][:].bitcast(FP8X4),
+                    rhs_scale=x_scale[a][g][:],
                     start=(a == 0),
                     stop=(a == last),
                 )
 
-        def finish(g):
-            lo, hi = GROUPS[g]
-            nc.scalar.activation(result[:, 0, lo:hi], acc[g, 0][:, : hi - lo], RELU, bias=bias[:, 0:1])
-            nc.vector.tensor_scalar(result[:, 1, lo:hi], acc[g, 1][:, : hi - lo], bias[:, 1:2], 0.0, ADD, MAX)
+        def finish_on_scalar(g, m):
+            nc.scalar.activation(result[g][:, m, :], acc[g][m][:, :THIRD], RELU, bias=bias[:, m : m + 1])
 
-        def store(lo, hi):
+        def finish_on_vector(g, m):
+            nc.vector.tensor_scalar(result[g][:, m, :], acc[g][m][:, :THIRD], bias[:, m : m + 1], 0.0, ADD, MAX)
+
+        def store(g):
             rows = out.rearrange("(m p) n -> p m n", p=P)
-            nc.sync.dma_start(out=rows[:, :, lo:hi], in_=result[:, :, lo:hi])
+            nc.sync.dma_start(out=rows[:, :, g * THIRD : (g + 1) * THIRD], in_=result[g][:])
 
-        thirds = [(lo, lo + THIRD) for lo in range(0, S, THIRD)]
+        def pair(a, t):
+            both = [keep.tile([P, 2, THIRD], F32, name=f"both{a}_{t}_{g}", align_bytes=64) for g in thirds]
+            for g in thirds:
+                on_scalar(both[g][:, 0, :], third(a, t, g))
+            for g in thirds[:2]:
+                on_vector(both[g][:, 1, :], third(a, t + 1, g))
+            on_scalar(both[2][:, 1, :], third(a, t + 1, 2))
+            for g in thirds:
+                on_vector(grouped[a][g][:, :, t : t + 2], both[g][:].rearrange("p t n -> p n t"))
 
-        for a in range(PASSES):
-            if a == 0:
-                gather(a, 0, 0, S)
-            else:
-                gather_on_scalar(a)
-            if 0 < a < last:
-                quantize_into(a - 1, THIRD, S, f"plane{a}_0")
-            if a == last:
-                quantize_into(a - 1, *GROUPS[1], f"plane{a}_0")
-            gather(a, 1, 0, S)
-            if a == last:
-                new_codes(a - 1, GROUPS[2][0], S, f"plane{a}_1")
-                quantize(a - 1, *GROUPS[2])
-                quantize(a - 1, *GROUPS[3])
-            interleave(a, 0, 0, S)
-            if a < last:
-                gather(a, 2, 0, S)
-                for lo, hi in thirds:
-                    gather(a, 3, lo, hi)
-                    interleave(a, 1, lo, hi)
-                quantize_into(a, 0, THIRD, f"x_codes{a}_0")
-
-        for lo, hi in thirds[:2]:
-            gather(last, 2, lo, hi)
-        gather_grouped(last, 2, *GROUPS[3])
-        for lo, hi in thirds[:2]:
-            gather(last, 3, lo, hi)
-        for lo, hi in GROUPS[:3]:
-            interleave(last, 1, lo, hi)
-        gather_grouped(last, 3, *GROUPS[3])
-        quantize_into(last, *GROUPS[0], "x_codes_first")
-        quantize_into(last, *GROUPS[3], "high_head")
-        quantize_into(last, *GROUPS[1], "x_codes_third")
-        quantize_into(last, *GROUPS[2], "x_codes_last")
-
-        for a in range(PASSES):
-            for g in FINISH_ORDER:
-                multiply(a, g)
-        for g in FINISH_ORDER:
-            finish(g)
-        store(0, THIRD)
-        store(THIRD, S)
+        for a in range(last):
+            pair(a, 0)
+            pair(a, 2)
+            for g in thirds:
+                quantize(a, g, 0, THIRD)
+        three = [keep.tile([P, 3, THIRD], F32, name=f"three{g}", align_bytes=64) for g in thirds]
+        for g in thirds:
+            on_scalar(three[g][:, 0, :], third(last, 0, g))
+            on_vector(three[g][:, 1, :], third(last, 1, g))
+        on_vector(grouped[last][0][:, :, 0:2], three[0][:, 0:2, :].rearrange("p t n -> p n t"))
+        on_vector(grouped[last][0][:, :, 2], third(last, 2, 0))
+        for g in thirds[1:]:
+            on_scalar(three[g][:, 2, :], third(last, 2, g))
+            on_vector(grouped[last][g][:, :, 0:3], three[g][:].rearrange("p t n -> p n t"))
+        for g in thirds:
+            multiply(0, g)
+        head = keep.tile([P, P], BF16, name="head", align_bytes=64)
+        second = keep.tile([P, P], BF16, name="second", align_bytes=64)
+        runs = [keep.tile([P, THIRD], BF16, name=f"run3_{g}", align_bytes=64) for g in thirds[1:]]
+        on_vector(head[:], window(last, 3, P, 2 * P))
+        on_scalar(second[:], window(last, 3, 0, P))
+        for g in thirds[1:]:
+            on_scalar(runs[g - 1][:], third(last, 3, g))
+        halves = [[second[:], head[:]]] + [[run[:, :P], run[:, P:]] for run in runs]
+        for g in thirds:
+            for h in range(2):
+                on_vector(grouped[last][g][:, h * P : (h + 1) * P, 3], halves[g][h])
+            for h in range(2):
+                quantize(last, g, h * P, (h + 1) * P)
+            multiply(1, g)
+            multiply(last, g)
+        finish_on_scalar(0, 0)
+        finish_on_scalar(0, 1)
+        store(0)
+        for g in thirds[1:]:
+            finish_on_scalar(g, 0)
+            finish_on_vector(g, 1)
+            store(g)

@@ -26,7 +26,7 @@ PER_COL = 16
 QUADRANT = 32
 SCALE_ROWS = 4
 BANK = 512
-LOADS = [(0, 0, 2), (0, 2, 2), (1, 0, 2), (1, 2, 2), (2, 0, 2), (2, 2, 1), (2, 3, 1)]
+LOADS = [(0, 0, 4), (1, 0, 2), (1, 2, 2), (2, 0, 2), (2, 2, 1), (2, 3, 1)]
 
 
 def tile_picked_pick_lin_relu_sub_e_kernel(tc, xT, w_words, w_scales, b, offs, out):
@@ -76,7 +76,7 @@ def tile_picked_pick_lin_relu_sub_e_kernel(tc, xT, w_words, w_scales, b, offs, o
         x_codes = [[keep.tile([P, THIRD], U32, name=f"x_codes{a}_{g}", align_bytes=64) for g in thirds] for a in range(PASSES)]
         x_scale = [[keep.tile([P, THIRD], U8, name=f"x_scale{a}_{g}", align_bytes=64) for g in thirds] for a in range(PASSES)]
         acc = [[psum.tile([P, BANK], F32, name=f"acc{g}_{m}") for m in range(M_TILES)] for g in thirds]
-        result = [keep.tile([P, M_TILES, THIRD], F32, name=f"result{g}") for g in thirds]
+        result = [[keep.tile([P, THIRD], F32, name=f"result{g}_{m}") for m in range(M_TILES)] for g in thirds]
 
         def window(a, t, lo, hi):
             return plane[a, t].indirect(offsets[:, lo // PER_COL : hi // PER_COL])
@@ -111,30 +111,37 @@ def tile_picked_pick_lin_relu_sub_e_kernel(tc, xT, w_words, w_scales, b, offs, o
                 )
 
         def finish_on_scalar(g, m):
-            nc.scalar.activation(result[g][:, m, :], acc[g][m][:, :THIRD], RELU, bias=bias[:, m : m + 1])
+            nc.scalar.activation(result[g][m][:], acc[g][m][:, :THIRD], RELU, bias=bias[:, m : m + 1])
 
         def finish_on_vector(g, m):
-            nc.vector.tensor_scalar(result[g][:, m, :], acc[g][m][:, :THIRD], bias[:, m : m + 1], 0.0, ADD, MAX)
+            nc.vector.tensor_scalar(result[g][m][:], acc[g][m][:, :THIRD], bias[:, m : m + 1], 0.0, ADD, MAX)
 
-        def store(g):
-            rows = out.rearrange("(m p) n -> p m n", p=P)
-            nc.sync.dma_start(out=rows[:, :, g * THIRD : (g + 1) * THIRD], in_=result[g][:])
+        def store(g, m):
+            nc.sync.dma_start(out=out[m * P : (m + 1) * P, g * THIRD : (g + 1) * THIRD], in_=result[g][m][:])
 
-        def pair(a, t):
-            both = [keep.tile([P, 2, THIRD], F32, name=f"both{a}_{t}_{g}", align_bytes=64) for g in thirds]
+        picked = [[keep.tile([P, PACK, THIRD], F32, name=f"picked{a}_{g}", align_bytes=64) for g in thirds] for a in range(last)]
+
+        def interleave(a, g):
+            on_vector(grouped[a][g][:], picked[a][g][:].rearrange("p t n -> p n t"))
+
+        for g in thirds:
+            for t in range(2):
+                on_scalar(picked[0][g][:, t, :], third(0, t, g))
+                on_vector(picked[0][g][:, 2 + t, :], third(0, 2 + t, g))
+        for g in thirds:
+            interleave(0, g)
+        for g in thirds:
+            quantize(0, g, 0, THIRD)
+        for t in (0, 2):
             for g in thirds:
-                on_scalar(both[g][:, 0, :], third(a, t, g))
+                on_scalar(picked[1][g][:, t, :], third(1, t, g))
             for g in thirds[:2]:
-                on_vector(both[g][:, 1, :], third(a, t + 1, g))
-            on_scalar(both[2][:, 1, :], third(a, t + 1, 2))
-            for g in thirds:
-                on_vector(grouped[a][g][:, :, t : t + 2], both[g][:].rearrange("p t n -> p n t"))
-
-        for a in range(last):
-            pair(a, 0)
-            pair(a, 2)
-            for g in thirds:
-                quantize(a, g, 0, THIRD)
+                on_vector(picked[1][g][:, t + 1, :], third(1, t + 1, g))
+            on_scalar(picked[1][2][:, t + 1, :], third(1, t + 1, 2))
+        for g in thirds:
+            interleave(1, g)
+        for g in thirds:
+            quantize(1, g, 0, THIRD)
         three = [keep.tile([P, 3, THIRD], F32, name=f"three{g}", align_bytes=64) for g in thirds]
         for g in thirds:
             on_scalar(three[g][:, 0, :], third(last, 0, g))
@@ -146,25 +153,26 @@ def tile_picked_pick_lin_relu_sub_e_kernel(tc, xT, w_words, w_scales, b, offs, o
             on_vector(grouped[last][g][:, :, 0:3], three[g][:].rearrange("p t n -> p n t"))
         for g in thirds:
             multiply(0, g)
-        head = keep.tile([P, P], BF16, name="head", align_bytes=64)
-        second = keep.tile([P, P], BF16, name="second", align_bytes=64)
-        runs = [keep.tile([P, THIRD], BF16, name=f"run3_{g}", align_bytes=64) for g in thirds[1:]]
-        on_vector(head[:], window(last, 3, P, 2 * P))
-        on_scalar(second[:], window(last, 3, 0, P))
-        for g in thirds[1:]:
-            on_scalar(runs[g - 1][:], third(last, 3, g))
-        halves = [[second[:], head[:]]] + [[run[:, :P], run[:, P:]] for run in runs]
+        halves = [keep.tile([P, P], BF16, name=f"half{h}", align_bytes=64) for h in range(4)]
+        on_vector(grouped[last][0][:, :, 3], third(last, 3, 0))
+        for h in range(4):
+            on_scalar(halves[h][:], window(last, 3, THIRD + h * P, THIRD + (h + 1) * P))
+        on_vector(grouped[last][1][:, :P, 3], halves[0][:])
+        quantize(last, 0, 0, THIRD)
+        on_vector(grouped[last][1][:, P:, 3], halves[1][:])
+        on_vector(grouped[last][2][:, :P, 3], halves[2][:])
+        quantize(last, 1, 0, THIRD)
+        on_vector(grouped[last][2][:, P:, 3], halves[3][:])
+        quantize(last, 2, 0, P)
+        quantize(last, 2, P, THIRD)
         for g in thirds:
-            for h in range(2):
-                on_vector(grouped[last][g][:, h * P : (h + 1) * P, 3], halves[g][h])
-            for h in range(2):
-                quantize(last, g, h * P, (h + 1) * P)
             multiply(1, g)
             multiply(last, g)
-        finish_on_scalar(0, 0)
-        finish_on_scalar(0, 1)
-        store(0)
-        for g in thirds[1:]:
+        for g in thirds:
             finish_on_scalar(g, 0)
-            finish_on_vector(g, 1)
-            store(g)
+            store(g, 0)
+            if g == 0:
+                finish_on_scalar(g, 1)
+            else:
+                finish_on_vector(g, 1)
+            store(g, 1)

@@ -121,8 +121,11 @@ def tile_picked_pick_lin_relu_sub_e_kernel(tc, xT, w_words, w_scales, b, offs, o
 
         picked = [[keep.tile([P, PACK, THIRD], F32, name=f"picked{a}_{g}", align_bytes=64) for g in thirds] for a in range(last)]
 
+        def place(copy, dst, src):
+            copy(dst.rearrange("p (c i) t -> p c t i", i=PACK), src.rearrange("p t (c i) -> p c t i", i=PACK))
+
         def interleave(a, g):
-            on_vector(grouped[a][g][:], picked[a][g][:].rearrange("p t n -> p n t"))
+            place(on_vector, grouped[a][g][:], picked[a][g][:])
 
         for g in thirds:
             for t in range(2):
@@ -138,19 +141,23 @@ def tile_picked_pick_lin_relu_sub_e_kernel(tc, xT, w_words, w_scales, b, offs, o
             for g in thirds[:2]:
                 on_vector(picked[1][g][:, t + 1, :], third(1, t + 1, g))
             on_scalar(picked[1][2][:, t + 1, :], third(1, t + 1, 2))
-        for g in thirds:
+        for g in thirds[:2]:
             interleave(1, g)
+        place(on_vector, grouped[1][2][:, :P, :], picked[1][2][:, :, :P])
+        place(on_scalar, grouped[1][2][:, P:, :], picked[1][2][:, :, P:])
         for g in thirds:
             quantize(1, g, 0, THIRD)
         three = [keep.tile([P, 3, THIRD], F32, name=f"three{g}", align_bytes=64) for g in thirds]
         for g in thirds:
             on_scalar(three[g][:, 0, :], third(last, 0, g))
             on_vector(three[g][:, 1, :], third(last, 1, g))
-        on_vector(grouped[last][0][:, :, 0:2], three[0][:, 0:2, :].rearrange("p t n -> p n t"))
+        place(on_vector, grouped[last][0][:, :, 0:2], three[0][:, 0:2, :])
         on_vector(grouped[last][0][:, :, 2], third(last, 2, 0))
         for g in thirds[1:]:
             on_scalar(three[g][:, 2, :], third(last, 2, g))
-            on_vector(grouped[last][g][:, :, 0:3], three[g][:].rearrange("p t n -> p n t"))
+        place(on_vector, grouped[last][1][:, :, 0:3], three[1][:])
+        place(on_vector, grouped[last][2][:, :P, 0:3], three[2][:, :, :P])
+        place(on_scalar, grouped[last][2][:, P:, 0:3], three[2][:, :, P:])
         for g in thirds:
             multiply(0, g)
         halves = [keep.tile([P, P], BF16, name=f"half{h}", align_bytes=64) for h in range(4)]

@@ -75,7 +75,8 @@ def tile_picked_pick_lin_relu_sub_e_kernel(tc, xT, w_words, w_scales, b, offs, o
         grouped = [[keep.tile([P, THIRD, PACK], BF16, name=f"grouped{a}_{g}", align_bytes=64) for g in thirds] for a in range(PASSES)]
         x_codes = [[keep.tile([P, THIRD], U32, name=f"x_codes{a}_{g}", align_bytes=64) for g in thirds] for a in range(PASSES)]
         x_scale = [[keep.tile([P, THIRD], U8, name=f"x_scale{a}_{g}", align_bytes=64) for g in thirds] for a in range(PASSES)]
-        acc = [[psum.tile([P, BANK], F32, name=f"acc{g}_{m}") for m in range(M_TILES)] for g in thirds]
+        spans = {(g, m): [(0, P), (P, THIRD)] if m == 0 and g < 2 else [(0, THIRD)] for g in thirds for m in range(M_TILES)}
+        acc = {(g, m, lo): psum.tile([P, BANK], F32, name=f"acc{g}_{m}_{lo}") for (g, m), parts in spans.items() for lo, hi in parts}
         result = [[keep.tile([P, THIRD], F32, name=f"result{g}_{m}") for m in range(M_TILES)] for g in thirds]
 
         def window(a, t, lo, hi):
@@ -100,21 +101,23 @@ def tile_picked_pick_lin_relu_sub_e_kernel(tc, xT, w_words, w_scales, b, offs, o
         def multiply(a, g):
             for m in range(M_TILES):
                 cols = slice(m * P, (m + 1) * P)
-                nc.tensor.matmul_mx(
-                    out=acc[g][m][:, :THIRD],
-                    lhsT=w_codes[a][:, cols].bitcast(FP8X4),
-                    lhsT_scale=w_scale[:, a, cols],
-                    rhs=x_codes[a][g][:].bitcast(FP8X4),
-                    rhs_scale=x_scale[a][g][:],
-                    start=(a == 0),
-                    stop=(a == last),
-                )
+                for lo, hi in spans[g, m]:
+                    nc.tensor.matmul_mx(
+                        out=acc[g, m, lo][:, : hi - lo],
+                        lhsT=w_codes[a][:, cols].bitcast(FP8X4),
+                        lhsT_scale=w_scale[:, a, cols],
+                        rhs=x_codes[a][g][:, lo:hi].bitcast(FP8X4),
+                        rhs_scale=x_scale[a][g][:, lo:hi],
+                        start=(a == 0),
+                        stop=(a == last),
+                    )
 
         def finish_on_scalar(g, m):
-            nc.scalar.activation(result[g][m][:], acc[g][m][:, :THIRD], RELU, bias=bias[:, m : m + 1])
+            for lo, hi in spans[g, m]:
+                nc.scalar.activation(result[g][m][:, lo:hi], acc[g, m, lo][:, : hi - lo], RELU, bias=bias[:, m : m + 1])
 
         def finish_on_vector(g, m):
-            nc.vector.tensor_scalar(result[g][m][:], acc[g][m][:, :THIRD], bias[:, m : m + 1], 0.0, ADD, MAX)
+            nc.vector.tensor_scalar(result[g][m][:], acc[g, m, 0][:, :THIRD], bias[:, m : m + 1], 0.0, ADD, MAX)
 
         def store(g, m):
             nc.sync.dma_start(out=out[m * P : (m + 1) * P, g * THIRD : (g + 1) * THIRD], in_=result[g][m][:])
@@ -162,16 +165,17 @@ def tile_picked_pick_lin_relu_sub_e_kernel(tc, xT, w_words, w_scales, b, offs, o
             multiply(0, g)
         halves = [keep.tile([P, P], BF16, name=f"half{h}", align_bytes=64) for h in range(4)]
         on_vector(grouped[last][0][:, :, 3], third(last, 3, 0))
-        for h in range(4):
+        for h in (0, 1, 3, 2):
             on_scalar(halves[h][:], window(last, 3, THIRD + h * P, THIRD + (h + 1) * P))
+        on_scalar(grouped[last][2][:, P:, 3], halves[3][:])
         on_vector(grouped[last][1][:, :P, 3], halves[0][:])
-        quantize(last, 0, 0, THIRD)
+        quantize(last, 0, 0, P)
+        quantize(last, 0, P, THIRD)
         on_vector(grouped[last][1][:, P:, 3], halves[1][:])
         on_vector(grouped[last][2][:, :P, 3], halves[2][:])
-        quantize(last, 1, 0, THIRD)
-        on_vector(grouped[last][2][:, P:, 3], halves[3][:])
-        quantize(last, 2, 0, P)
-        quantize(last, 2, P, THIRD)
+        quantize(last, 1, 0, P)
+        quantize(last, 1, P, THIRD)
+        quantize(last, 2, 0, THIRD)
         for g in thirds:
             multiply(1, g)
             multiply(last, g)

@@ -60,14 +60,19 @@ def tile_picked_pick_lin_relu_sub_e_kernel(tc, xT, w_words, w_scales, b, offs, o
         nc.sync.dma_start(offsets[:], offs)
         load_planes(*LOADS[1])
         scale_rows = w_scales.rearrange("a (q r) m -> r q a m", r=SCALE_ROWS).bitcast(I32)
-        for r in range(SCALE_ROWS):
-            nc.sync.dma_start(out=w_scale[r:P:QUADRANT].bitcast(I32), in_=scale_rows[r])
+
+        def load_scales(passes):
+            for r in range(SCALE_ROWS):
+                nc.sync.dma_start(out=w_scale[r:P:QUADRANT, passes].bitcast(I32), in_=scale_rows[r][:, passes])
+
+        load_scales(slice(0, last))
         for load in LOADS[2:-1]:
             load_planes(*load)
         load_codes(0)
         load_planes(*LOADS[-1])
         load_codes(1)
         load_codes(2)
+        load_scales(slice(last, PASSES))
         with nc.allow_non_contiguous_dma(reason="one bias value a partition and output tile"):
             nc.sync.dma_start(out=bias[:], in_=b.rearrange("(c p) o -> p (c o)", p=P))
 
@@ -77,7 +82,7 @@ def tile_picked_pick_lin_relu_sub_e_kernel(tc, xT, w_words, w_scales, b, offs, o
         x_scale = [[keep.tile([P, THIRD], U8, name=f"x_scale{a}_{g}", align_bytes=64) for g in thirds] for a in range(PASSES)]
         spans = {(g, m): [(0, P), (P, THIRD)] if m == 0 and g < 2 else [(0, THIRD)] for g in thirds for m in range(M_TILES)}
         acc = {(g, m, lo): psum.tile([P, BANK], F32, name=f"acc{g}_{m}_{lo}") for (g, m), parts in spans.items() for lo, hi in parts}
-        result = [[keep.tile([P, THIRD], F32, name=f"result{g}_{m}") for m in range(M_TILES)] for g in thirds]
+        result = [keep.tile([P, M_TILES, THIRD], F32, name=f"result{g}") for g in thirds]
 
         def window(a, t, lo, hi):
             return plane[a, t].indirect(offsets[:, lo // PER_COL : hi // PER_COL])
@@ -114,13 +119,13 @@ def tile_picked_pick_lin_relu_sub_e_kernel(tc, xT, w_words, w_scales, b, offs, o
 
         def finish_on_scalar(g, m):
             for lo, hi in spans[g, m]:
-                nc.scalar.activation(result[g][m][:, lo:hi], acc[g, m, lo][:, : hi - lo], RELU, bias=bias[:, m : m + 1])
+                nc.scalar.activation(result[g][:, m, lo:hi], acc[g, m, lo][:, : hi - lo], RELU, bias=bias[:, m : m + 1])
 
         def finish_on_vector(g, m):
-            nc.vector.tensor_scalar(result[g][m][:], acc[g, m, 0][:, :THIRD], bias[:, m : m + 1], 0.0, ADD, MAX)
+            nc.vector.tensor_scalar(result[g][:, m, :], acc[g, m, 0][:, :THIRD], bias[:, m : m + 1], 0.0, ADD, MAX)
 
         def store(g, m):
-            nc.sync.dma_start(out=out[m * P : (m + 1) * P, g * THIRD : (g + 1) * THIRD], in_=result[g][m][:])
+            nc.sync.dma_start(out=out[m * P : (m + 1) * P, g * THIRD : (g + 1) * THIRD], in_=result[g][:, m, :])
 
         picked = [[keep.tile([P, PACK, THIRD], F32, name=f"picked{a}_{g}", align_bytes=64) for g in thirds] for a in range(last)]
 
@@ -179,11 +184,13 @@ def tile_picked_pick_lin_relu_sub_e_kernel(tc, xT, w_words, w_scales, b, offs, o
         for g in thirds:
             multiply(1, g)
             multiply(last, g)
-        for g in thirds:
-            finish_on_scalar(g, 0)
-            store(g, 0)
-            if g == 0:
-                finish_on_scalar(g, 1)
-            else:
-                finish_on_vector(g, 1)
-            store(g, 1)
+        for m in range(M_TILES):
+            finish_on_scalar(0, m)
+            store(0, m)
+        finish_on_scalar(1, 0)
+        store(1, 0)
+        finish_on_vector(1, 1)
+        store(1, 1)
+        finish_on_scalar(2, 0)
+        finish_on_vector(2, 1)
+        nc.sync.dma_start(out=out.rearrange("(m p) n -> p m n", p=P)[:, :, 2 * THIRD :], in_=result[2][:])

@@ -80,9 +80,12 @@ def tile_picked_pick_lin_relu_sub_e_kernel(tc, xT, w_words, w_scales, b, offs, o
         grouped = [[keep.tile([P, THIRD, PACK], BF16, name=f"grouped{a}_{g}", align_bytes=64) for g in thirds] for a in range(PASSES)]
         x_codes = [[keep.tile([P, THIRD], U32, name=f"x_codes{a}_{g}", align_bytes=64) for g in thirds] for a in range(PASSES)]
         x_scale = [[keep.tile([P, THIRD], U8, name=f"x_scale{a}_{g}", align_bytes=64) for g in thirds] for a in range(PASSES)]
-        spans = {(g, m): [(0, P), (P, THIRD)] if m == 0 and g < 2 else [(0, THIRD)] for g in thirds for m in range(M_TILES)}
+        spans = {(g, m): [(0, P), (P, THIRD)] if m == 0 and g != 1 else [(0, THIRD)] for g in thirds for m in range(M_TILES)}
         acc = {(g, m, lo): psum.tile([P, BANK], F32, name=f"acc{g}_{m}_{lo}") for (g, m), parts in spans.items() for lo, hi in parts}
-        result = [keep.tile([P, M_TILES, THIRD], F32, name=f"result{g}") for g in thirds]
+        upper = [keep.tile([P, THIRD], F32, name=f"upper{g}") for g in thirds[:2]]
+        lower = keep.tile([P, 2 * THIRD], F32, name="lower")
+        closing = keep.tile([P, M_TILES, THIRD], F32, name="closing")
+        result = {(0, 0): upper[0][:], (1, 0): upper[1][:], (0, 1): lower[:, :THIRD], (1, 1): lower[:, THIRD:], (2, 0): closing[:, 0, :], (2, 1): closing[:, 1, :]}
 
         def window(a, t, lo, hi):
             return plane[a, t].indirect(offsets[:, lo // PER_COL : hi // PER_COL])
@@ -104,28 +107,30 @@ def tile_picked_pick_lin_relu_sub_e_kernel(tc, xT, w_words, w_scales, b, offs, o
             )
 
         def multiply(a, g):
-            for m in range(M_TILES):
+            parts = [(m, lo, hi) for m in range(M_TILES) for lo, hi in spans[g, m]]
+            if g == 2:
+                parts = [parts[0], parts[2], parts[1]]
+            for m, lo, hi in parts:
                 cols = slice(m * P, (m + 1) * P)
-                for lo, hi in spans[g, m]:
-                    nc.tensor.matmul_mx(
-                        out=acc[g, m, lo][:, : hi - lo],
-                        lhsT=w_codes[a][:, cols].bitcast(FP8X4),
-                        lhsT_scale=w_scale[:, a, cols],
-                        rhs=x_codes[a][g][:, lo:hi].bitcast(FP8X4),
-                        rhs_scale=x_scale[a][g][:, lo:hi],
-                        start=(a == 0),
-                        stop=(a == last),
-                    )
+                nc.tensor.matmul_mx(
+                    out=acc[g, m, lo][:, : hi - lo],
+                    lhsT=w_codes[a][:, cols].bitcast(FP8X4),
+                    lhsT_scale=w_scale[:, a, cols],
+                    rhs=x_codes[a][g][:, lo:hi].bitcast(FP8X4),
+                    rhs_scale=x_scale[a][g][:, lo:hi],
+                    start=(a == 0),
+                    stop=(a == last),
+                )
 
         def finish_on_scalar(g, m):
             for lo, hi in spans[g, m]:
-                nc.scalar.activation(result[g][:, m, lo:hi], acc[g, m, lo][:, : hi - lo], RELU, bias=bias[:, m : m + 1])
+                nc.scalar.activation(result[g, m][:, lo:hi], acc[g, m, lo][:, : hi - lo], RELU, bias=bias[:, m : m + 1])
 
         def finish_on_vector(g, m):
-            nc.vector.tensor_scalar(result[g][:, m, :], acc[g, m, 0][:, :THIRD], bias[:, m : m + 1], 0.0, ADD, MAX)
+            nc.vector.tensor_scalar(result[g, m], acc[g, m, 0][:, :THIRD], bias[:, m : m + 1], 0.0, ADD, MAX)
 
-        def store(g, m):
-            nc.sync.dma_start(out=out[m * P : (m + 1) * P, g * THIRD : (g + 1) * THIRD], in_=result[g][:, m, :])
+        def store_upper(g):
+            nc.sync.dma_start(out=out[:P, g * THIRD : (g + 1) * THIRD], in_=upper[g][:])
 
         picked = [[keep.tile([P, PACK, THIRD], F32, name=f"picked{a}_{g}", align_bytes=64) for g in thirds] for a in range(last)]
 
@@ -161,36 +166,44 @@ def tile_picked_pick_lin_relu_sub_e_kernel(tc, xT, w_words, w_scales, b, offs, o
             on_vector(three[g][:, 1, :], third(last, 1, g))
         place(on_vector, grouped[last][0][:, :, 0:2], three[0][:, 0:2, :])
         on_vector(grouped[last][0][:, :, 2], third(last, 2, 0))
-        for g in thirds[1:]:
+        for g in (2, 1):
             on_scalar(three[g][:, 2, :], third(last, 2, g))
-        place(on_vector, grouped[last][1][:, :, 0:3], three[1][:])
-        place(on_vector, grouped[last][2][:, :P, 0:3], three[2][:, :, :P])
-        place(on_scalar, grouped[last][2][:, P:, 0:3], three[2][:, :, P:])
+        place(on_scalar, grouped[last][1][:, :P, 0:3], three[1][:, :, :P])
+        place(on_vector, grouped[last][1][:, P:, 0:3], three[1][:, :, P:])
+        place(on_vector, grouped[last][2][:, :, 0:3], three[2][:])
         for g in thirds:
             multiply(0, g)
-        halves = [keep.tile([P, P], BF16, name=f"half{h}", align_bytes=64) for h in range(4)]
+        halves = [keep.tile([P, P], BF16, name=f"half{h}", align_bytes=64) for h in range(2)]
+
+        def gather_half(h):
+            on_scalar(halves[h % 2][:], window(last, 3, THIRD + h * P, THIRD + (h + 1) * P))
+
+        def place_half(copy, h):
+            copy(grouped[last][1 + h // 2][:, (h % 2) * P : (h % 2 + 1) * P, 3], halves[h % 2][:])
+
         on_vector(grouped[last][0][:, :, 3], third(last, 3, 0))
-        for h in (0, 1, 3, 2):
-            on_scalar(halves[h][:], window(last, 3, THIRD + h * P, THIRD + (h + 1) * P))
-        on_scalar(grouped[last][2][:, P:, 3], halves[3][:])
-        on_vector(grouped[last][1][:, :P, 3], halves[0][:])
-        quantize(last, 0, 0, P)
-        quantize(last, 0, P, THIRD)
-        on_vector(grouped[last][1][:, P:, 3], halves[1][:])
-        on_vector(grouped[last][2][:, :P, 3], halves[2][:])
-        quantize(last, 1, 0, P)
-        quantize(last, 1, P, THIRD)
-        quantize(last, 2, 0, THIRD)
+        gather_half(0)
+        gather_half(1)
+        place_half(on_scalar, 0)
+        place_half(on_vector, 1)
+        gather_half(2)
+        gather_half(3)
+        for g in thirds[:2]:
+            quantize(last, g, 0, P)
+            quantize(last, g, P, THIRD)
+        place_half(on_vector, 2)
+        place_half(on_vector, 3)
+        quantize(last, 2, 0, P)
+        quantize(last, 2, P, THIRD)
         for g in thirds:
             multiply(1, g)
             multiply(last, g)
-        for m in range(M_TILES):
-            finish_on_scalar(0, m)
-            store(0, m)
-        finish_on_scalar(1, 0)
-        store(1, 0)
+        for g in thirds[:2]:
+            finish_on_scalar(g, 0)
+            store_upper(g)
+        finish_on_scalar(0, 1)
         finish_on_vector(1, 1)
-        store(1, 1)
+        nc.sync.dma_start(out=out[P:, : 2 * THIRD], in_=lower[:])
         finish_on_scalar(2, 0)
         finish_on_vector(2, 1)
-        nc.sync.dma_start(out=out.rearrange("(m p) n -> p m n", p=P)[:, :, 2 * THIRD :], in_=result[2][:])
+        nc.sync.dma_start(out=out.rearrange("(m p) n -> p m n", p=P)[:, :, 2 * THIRD :], in_=closing[:])

@@ -36,9 +36,9 @@ def tile_picked_pick_lin_relu_sub_e_kernel(tc, xT, w_words, w_scales, b, offs, o
         keep = ctx.enter_context(tc.tile_pool(name="keep", bufs=1))
         psum = ctx.enter_context(tc.psum_pool(name="psum", bufs=1))
 
-        offsets = keep.tile([P, S // PER_COL], U16, name="offsets")
-        w_codes = [keep.tile([P, N], U32, name=f"w_codes{a}", align_bytes=64) for a in range(PASSES)]
-        w_scale = keep.tile([P, PASSES, N], U8, name="w_scale", align_bytes=64)
+        offsets = keep.tile([P, S // PER_COL], U16, name="offsets", align_bytes=256)
+        w_codes = [keep.tile([P, N], U32, name=f"w_codes{a}", align_bytes=256) for a in range(PASSES)]
+        w_scale = keep.tile([P, PASSES, N], U8, name="w_scale", align_bytes=256)
         bias = keep.tile([P, M_TILES], F32, name="bias")
 
         x_rows = xT.rearrange("(a p t) n -> a p (t n)", p=P, t=PACK)
@@ -46,7 +46,7 @@ def tile_picked_pick_lin_relu_sub_e_kernel(tc, xT, w_words, w_scales, b, offs, o
         plane = {}
 
         def load_planes(a, t0, count):
-            tile = keep.tile([P, count * T], F32, name=f"planes{a}_{t0}", align_bytes=64)
+            tile = keep.tile([P, count * T], F32, name=f"planes{a}_{t0}", align_bytes=256)
             nc.sync.dma_start(out=tile[:], in_=x_rows[a, :, t0 * T : (t0 + count) * T])
             for t in range(count):
                 plane[a, t0 + t] = tile[:, t * T : (t + 1) * T]
@@ -82,9 +82,9 @@ def tile_picked_pick_lin_relu_sub_e_kernel(tc, xT, w_words, w_scales, b, offs, o
         x_scale = [[keep.tile([P, THIRD], U8, name=f"x_scale{a}_{g}", align_bytes=64) for g in thirds] for a in range(PASSES)]
         spans = {(g, m): [(0, P), (P, THIRD)] if m == 0 and g != 1 else [(0, THIRD)] for g in thirds for m in range(M_TILES)}
         acc = {(g, m, lo): psum.tile([P, BANK], F32, name=f"acc{g}_{m}_{lo}") for (g, m), parts in spans.items() for lo, hi in parts}
-        upper = [keep.tile([P, THIRD], F32, name=f"upper{g}") for g in thirds[:2]]
-        lower = keep.tile([P, 2 * THIRD], F32, name="lower")
-        closing = keep.tile([P, M_TILES, THIRD], F32, name="closing")
+        upper = [keep.tile([P, THIRD], F32, name=f"upper{g}", align_bytes=256) for g in thirds[:2]]
+        lower = keep.tile([P, 2 * THIRD], F32, name="lower", align_bytes=256)
+        closing = keep.tile([P, M_TILES, THIRD], F32, name="closing", align_bytes=256)
         result = {(0, 0): upper[0][:], (1, 0): upper[1][:], (0, 1): lower[:, :THIRD], (1, 1): lower[:, THIRD:], (2, 0): closing[:, 0, :], (2, 1): closing[:, 1, :]}
 
         def window(a, t, lo, hi):

@@ -26,7 +26,7 @@ PER_COL = 16
 QUADRANT = 32
 SCALE_ROWS = 4
 BANK = 512
-LOADS = [(0, 0, 4), (1, 0, 2), (1, 2, 2), (2, 0, 2), (2, 2, 1), (2, 3, 1)]
+LOADS = [(0, 0, 4), (1, 0, 2), (1, 2, 2), (2, 0, 1), (2, 1, 1), (2, 2, 1), (2, 3, 1)]
 
 
 def tile_picked_pick_lin_relu_sub_e_kernel(tc, xT, w_words, w_scales, b, offs, out):
@@ -154,20 +154,21 @@ def tile_picked_pick_lin_relu_sub_e_kernel(tc, xT, w_words, w_scales, b, offs, o
             for g in thirds[:2]:
                 on_vector(picked[1][g][:, t + 1, :], third(1, t + 1, g))
             on_scalar(picked[1][2][:, t + 1, :], third(1, t + 1, 2))
-        for g in thirds[:2]:
+        for g in thirds:
             interleave(1, g)
-        place(on_vector, grouped[1][2][:, :P, :], picked[1][2][:, :, :P])
-        place(on_scalar, grouped[1][2][:, P:, :], picked[1][2][:, :, P:])
         for g in thirds:
             quantize(1, g, 0, THIRD)
         three = [keep.tile([P, 3, THIRD], F32, name=f"three{g}", align_bytes=64) for g in thirds]
         for g in thirds:
             on_scalar(three[g][:, 0, :], third(last, 0, g))
+        for g in thirds[:2]:
             on_vector(three[g][:, 1, :], third(last, 1, g))
+        on_scalar(three[2][:, 1, :], third(last, 1, 2))
         place(on_vector, grouped[last][0][:, :, 0:2], three[0][:, 0:2, :])
         on_vector(grouped[last][0][:, :, 2], third(last, 2, 0))
-        for g in (2, 1):
-            on_scalar(three[g][:, 2, :], third(last, 2, g))
+        on_scalar(three[1][:, 2, :], third(last, 2, 1))
+        on_scalar(three[2][:, 2, :P], window(last, 2, 2 * THIRD, S - P))
+        on_vector(three[2][:, 2, P:], window(last, 2, S - P, S))
         place(on_scalar, grouped[last][1][:, :P, 0:3], three[1][:, :, :P])
         place(on_vector, grouped[last][1][:, P:, 0:3], three[1][:, :, P:])
         place(on_vector, grouped[last][2][:, :, 0:3], three[2][:])

from contextlib import ExitStack

import concourse.mybir as mybir

K, T, S, N = 1536, 2048, 768, 256
FLOPS = 2 * K * S * N

F32 = mybir.dt.float32
BF16 = mybir.dt.bfloat16
I32 = mybir.dt.int32
U32 = mybir.dt.uint32
U16 = mybir.dt.uint16
U8 = mybir.dt.uint8
FP8X4 = mybir.dt.float8_e4m3fn_x4
COPY = mybir.ActivationFunctionType.Copy
RELU = mybir.ActivationFunctionType.Relu
ADD = mybir.AluOpType.add
MAX = mybir.AluOpType.max

P = 128
PACK = 4
PASSES = K // (P * PACK)
THIRD = S // 3
M_TILES = N // P
PER_COL = 16
QUADRANT = 32
SCALE_ROWS = 4
BANK = 512
LOADS = [(0, 0, 4), (1, 0, 2), (1, 2, 2), (2, 0, 1), (2, 1, 1), (2, 2, 1), (2, 3, 1)]


def tile_picked_pick_lin_relu_sub_e_kernel(tc, xT, w_words, w_scales, b, offs, out):
    nc = tc.nc
    last = PASSES - 1
    with ExitStack() as ctx:
        keep = ctx.enter_context(tc.tile_pool(name="keep", bufs=1))
        psum = ctx.enter_context(tc.psum_pool(name="psum", bufs=1))

        offsets = keep.tile([P, S // PER_COL], U16, name="offsets", align_bytes=256)
        w_codes = [keep.tile([P, N], U32, name=f"w_codes{a}", align_bytes=256) for a in range(PASSES)]
        w_scale = keep.tile([P, PASSES, N], U8, name="w_scale", align_bytes=256)
        bias = keep.tile([P, M_TILES], F32, name="bias")

        x_rows = xT.rearrange("(a p t) n -> a p (t n)", p=P, t=PACK)
        w_rows = w_words.rearrange("a p m r -> a p (m r)").bitcast(I32)
        plane = {}

        def load_planes(a, t0, count):
            tile = keep.tile([P, count * T], F32, name=f"planes{a}_{t0}", align_bytes=256)
            nc.sync.dma_start(out=tile[:], in_=x_rows[a, :, t0 * T : (t0 + count) * T])
            for t in range(count):
                plane[a, t0 + t] = tile[:, t * T : (t + 1) * T]

        def load_codes(a):
            nc.sync.dma_start(out=w_codes[a][:].bitcast(I32), in_=w_rows[a])

        nc.vector.memset(w_scale[:].bitcast(I32), 0)

        load_planes(*LOADS[0])
        nc.sync.dma_start(offsets[:], offs)
        load_planes(*LOADS[1])
        scale_rows = w_scales.rearrange("a (q r) m -> r q a m", r=SCALE_ROWS).bitcast(I32)

        def load_scales(passes):
            for r in range(SCALE_ROWS):
                nc.sync.dma_start(out=w_scale[r:P:QUADRANT, passes].bitcast(I32), in_=scale_rows[r][:, passes])

        load_scales(slice(0, last))
        for load in LOADS[2:-1]:
            load_planes(*load)
        load_codes(0)
        load_planes(*LOADS[-1])
        load_codes(1)
        load_codes(2)
        load_scales(slice(last, PASSES))
        with nc.allow_non_contiguous_dma(reason="one bias value a partition and output tile"):
            nc.sync.dma_start(out=bias[:], in_=b.rearrange("(c p) o -> p (c o)", p=P))

        thirds = range(3)
        grouped = [[keep.tile([P, THIRD, PACK], BF16, name=f"grouped{a}_{g}", align_bytes=64) for g in thirds] for a in range(PASSES)]
        x_codes = [[keep.tile([P, THIRD], U32, name=f"x_codes{a}_{g}", align_bytes=64) for g in thirds] for a in range(PASSES)]
        x_scale = [[keep.tile([P, THIRD], U8, name=f"x_scale{a}_{g}", align_bytes=64) for g in thirds] for a in range(PASSES)]
        spans = {(g, m): [(0, P), (P, THIRD)] if m == 0 and g != 1 else [(0, THIRD)] for g in thirds for m in range(M_TILES)}
        acc = {(g, m, lo): psum.tile([P, BANK], F32, name=f"acc{g}_{m}_{lo}") for (g, m), parts in spans.items() for lo, hi in parts}
        upper = [keep.tile([P, THIRD], F32, name=f"upper{g}", align_bytes=256) for g in thirds[:2]]
        lower = keep.tile([P, 2 * THIRD], F32, name="lower", align_bytes=256)
        closing = keep.tile([P, M_TILES, THIRD], F32, name="closing", align_bytes=256)
        result = {(0, 0): upper[0][:], (1, 0): upper[1][:], (0, 1): lower[:, :THIRD], (1, 1): lower[:, THIRD:], (2, 0): closing[:, 0, :], (2, 1): closing[:, 1, :]}

        def window(a, t, lo, hi):
            return plane[a, t].indirect(offsets[:, lo // PER_COL : hi // PER_COL])

        def third(a, t, g):
            return window(a, t, g * THIRD, (g + 1) * THIRD)

        def on_vector(dst, src):
            nc.vector.tensor_copy(dst, src)

        def on_scalar(dst, src):
            nc.scalar.activation(dst, src, COPY)

        def quantize(a, g, lo, hi):
            nc.vector.quantize_mx(
                out=x_codes[a][g][:, lo:hi].bitcast(FP8X4),
                scales=x_scale[a][g][:, lo:hi],
                in_=grouped[a][g][:, lo:hi, :].rearrange("p n t -> p (n t)"),
            )

        def multiply(a, g):
            parts = [(m, lo, hi) for m in range(M_TILES) for lo, hi in spans[g, m]]
            if g == 2:
                parts = [parts[0], parts[2], parts[1]]
            for m, lo, hi in parts:
                cols = slice(m * P, (m + 1) * P)
                nc.tensor.matmul_mx(
                    out=acc[g, m, lo][:, : hi - lo],
                    lhsT=w_codes[a][:, cols].bitcast(FP8X4),
                    lhsT_scale=w_scale[:, a, cols],
                    rhs=x_codes[a][g][:, lo:hi].bitcast(FP8X4),
                    rhs_scale=x_scale[a][g][:, lo:hi],
                    start=(a == 0),
                    stop=(a == last),
                )

        def finish_on_scalar(g, m):
            for lo, hi in spans[g, m]:
                nc.scalar.activation(result[g, m][:, lo:hi], acc[g, m, lo][:, : hi - lo], RELU, bias=bias[:, m : m + 1])

        def finish_on_vector(g, m):
            nc.vector.tensor_scalar(result[g, m], acc[g, m, 0][:, :THIRD], bias[:, m : m + 1], 0.0, ADD, MAX)

        def store_upper(g):
            nc.sync.dma_start(out=out[:P, g * THIRD : (g + 1) * THIRD], in_=upper[g][:])

        picked = [[keep.tile([P, PACK, THIRD], F32, name=f"picked{a}_{g}", align_bytes=64) for g in thirds] for a in range(last)]

        def place(copy, dst, src):
            copy(dst.rearrange("p (c i) t -> p c t i", i=PACK), src.rearrange("p t (c i) -> p c t i", i=PACK))

        def interleave(a, g):
            place(on_vector, grouped[a][g][:], picked[a][g][:])

        for g in thirds:
            for t in range(2):
                on_scalar(picked[0][g][:, t, :], third(0, t, g))
                on_vector(picked[0][g][:, 2 + t, :], third(0, 2 + t, g))
        for g in thirds:
            interleave(0, g)
        for g in thirds:
            quantize(0, g, 0, THIRD)
        for t in (0, 2):
            for g in thirds:
                on_scalar(picked[1][g][:, t, :], third(1, t, g))
            for g in thirds[:2]:
                on_vector(picked[1][g][:, t + 1, :], third(1, t + 1, g))
            on_scalar(picked[1][2][:, t + 1, :], third(1, t + 1, 2))
        for g in thirds:
            interleave(1, g)
        for g in thirds:
            quantize(1, g, 0, THIRD)
        three = [keep.tile([P, 3, THIRD], F32, name=f"three{g}", align_bytes=64) for g in thirds]
        for g in thirds:
            on_scalar(three[g][:, 0, :], third(last, 0, g))
        for g in thirds[:2]:
            on_vector(three[g][:, 1, :], third(last, 1, g))
        on_scalar(three[2][:, 1, :], third(last, 1, 2))
        place(on_vector, grouped[last][0][:, :, 0:2], three[0][:, 0:2, :])
        on_vector(grouped[last][0][:, :, 2], third(last, 2, 0))
        on_scalar(three[1][:, 2, :], third(last, 2, 1))
        on_scalar(three[2][:, 2, :P], window(last, 2, 2 * THIRD, S - P))
        on_vector(three[2][:, 2, P:], window(last, 2, S - P, S))
        place(on_scalar, grouped[last][1][:, :P, 0:3], three[1][:, :, :P])
        place(on_vector, grouped[last][1][:, P:, 0:3], three[1][:, :, P:])
        place(on_vector, grouped[last][2][:, :, 0:3], three[2][:])
        for g in thirds:
            multiply(0, g)
        halves = [keep.tile([P, P], BF16, name=f"half{h}", align_bytes=64) for h in range(2)]

        def gather_half(h):
            on_scalar(halves[h % 2][:], window(last, 3, THIRD + h * P, THIRD + (h + 1) * P))

        def place_half(copy, h):
            copy(grouped[last][1 + h // 2][:, (h % 2) * P : (h % 2 + 1) * P, 3], halves[h % 2][:])

        on_vector(grouped[last][0][:, :, 3], third(last, 3, 0))
        gather_half(0)
        gather_half(1)
        place_half(on_scalar, 0)
        place_half(on_vector, 1)
        gather_half(2)
        gather_half(3)
        for g in thirds[:2]:
            quantize(last, g, 0, P)
            quantize(last, g, P, THIRD)
        place_half(on_vector, 2)
        place_half(on_vector, 3)
        quantize(last, 2, 0, P)
        quantize(last, 2, P, THIRD)
        for g in thirds:
            multiply(1, g)
            multiply(last, g)
        for g in thirds[:2]:
            finish_on_scalar(g, 0)
            store_upper(g)
        finish_on_scalar(0, 1)
        finish_on_vector(1, 1)
        nc.sync.dma_start(out=out[P:, : 2 * THIRD], in_=lower[:])
        finish_on_scalar(2, 0)
        finish_on_vector(2, 1)
        nc.sync.dma_start(out=out.rearrange("(m p) n -> p m n", p=P)[:, :, 2 * THIRD :], in_=closing[:])
